import numpy as np
import ml_dtypes


def mxq(x, axis, fmt="e4m3"):
    dtype, down = {"e4m3": (ml_dtypes.float8_e4m3fn, 7), "e5m2": (ml_dtypes.float8_e5m2, 14)}[fmt]
    v = np.moveaxis(np.asarray(x, np.float32).astype(ml_dtypes.bfloat16).astype(np.float64), axis, -1)
    blocks = v.reshape(v.shape[:-1] + (-1, 32))
    amax = np.abs(blocks).max(-1, keepdims=True)
    byte = np.maximum(np.where(amax > 0, np.frexp(amax)[1] - 1 + 127, 0) - down, 1)
    scale = np.exp2(byte - 127.0)
    codes = (blocks / scale).astype(np.float32).astype(dtype).astype(np.float64)
    return np.moveaxis((codes * scale).reshape(v.shape), -1, axis)


WIDE = False


def mx_kscale(k):
    if not WIDE:
        return np.ones(k)
    levels = np.array([10, -10, 5, -5, 0])
    if k % 512:
        return np.exp2(np.random.permutation(np.resize(levels, k // 32))).repeat(32)
    a = np.empty((k // 512, 16))
    for p in range(k // 512):
        a[p, :8] = np.random.permutation(np.resize(levels, 8))
        for g in range(8):
            far = levels[np.abs(levels - a[p, g]) >= 10]
            a[p, g + 8] = far[np.random.randint(len(far))]
    return np.exp2(a.ravel()).repeat(32)


def f64(x):
    return np.asarray(x).astype(np.float64)


def striped(idx):
    return np.tile(idx.reshape(-1, 16).T, (8, 1)).astype(np.uint16)


def unstriped(offs):
    return offs[:16].T.reshape(-1).astype(np.int64)


def gelu(v):
    return 0.5 * v * (1.0 + np.tanh(np.sqrt(2.0 / np.pi) * (v + 0.044715 * v**3)))


K, T, S, V, N = 1024, 1024, 512, 256, 128


def setup_inputs():
    n = np.random.standard_normal
    s = mx_kscale(K)[:, None]
    return {
        "xT": (n((K, T)) * s).astype(np.float32),
        "w1": (n((K, N)) / np.sqrt(K) / s).astype(np.float32),
        "offs": striped(np.random.permutation(T)[:S]),
        "pos1": striped(np.random.permutation(S)[:V]),
        "pos2": striped(np.random.permutation(S)[:V]),
        "pos3": striped(np.random.permutation(S)[:V]),
    }


def reference(xT, w1, offs, pos1, pos2, pos3):
    xq = mxq(f64(xT)[:, unstriped(offs)], 0, "e4m3")
    y = gelu(mxq(f64(w1), 0, "e4m3").T @ xq)
    n0 = y[:, unstriped(pos1)]
    n1 = y[:, unstriped(pos2)]
    n2 = y[:, unstriped(pos3)]
    return np.maximum(np.minimum(n0, n1), np.minimum(np.maximum(n0, n1), n2))

@@ -1,0 +1,132 @@
+from contextlib import ExitStack
+
+import concourse.mybir as mybir
+
+K, T, S, V, N = 1024, 1024, 512, 256, 128
+FLOPS = 2 * K * N * S
+
+F32 = mybir.dt.float32
+BF16 = mybir.dt.bfloat16
+U32 = mybir.dt.uint32
+U16 = mybir.dt.uint16
+U8 = mybir.dt.uint8
+FP8X4 = mybir.dt.float8_e4m3fn_x4
+ALU = mybir.AluOpType
+ACT = mybir.ActivationFunctionType
+
+P = 128
+PACK = 4
+K_PASS = P * PACK
+PASSES = K // K_PASS
+CHUNKS = (((512, 512), (512, 320)), ((512, 0), (512, 256)), ((512, 0), (512, 128)), ((512, 0), (256, 0), (256, 160)))
+PIECES = (256, 128, 128)
+
+
+def tile_picked_median_gelu_e_kernel(tc, xT, w1, offs, pos1, pos2, pos3, out):
+    nc = tc.nc
+    with ExitStack() as ctx:
+        keep = ctx.enter_context(tc.tile_pool(name="keep", bufs=1))
+        psum = ctx.enter_context(tc.psum_pool(name="psum", bufs=1))
+
+        offs_sb = keep.tile([P, S // 16], U16, name="offs_sb")
+        pos_sb = [keep.tile([P, V // 16], U16, name="pos_sb%d" % i) for i in range(3)]
+        x_rows = xT.rearrange("(z p j) t -> z p j t", p=P, j=PACK)
+        w_rows = w1.rearrange("(z p j) m -> z p j m", p=P, j=PACK)
+
+        raw = []
+        for q in range(4):
+            z, u = divmod(q, 2)
+            c0 = 0
+            row = []
+            for i, (cols, on_v) in enumerate(CHUNKS[q]):
+                t = keep.tile([P, 2, cols], F32, name="raw%d_%d" % (q, i), align_bytes=64)
+                nc.sync.dma_start(out=t[:], in_=x_rows[z, :, 2 * u : 2 * u + 2, c0 : c0 + cols])
+                if q == 0 and i == 0:
+                    nc.sync.dma_start(offs_sb[:], offs)
+                row.append((t, c0, cols, on_v))
+                c0 = c0 + cols
+            raw.append(row)
+        w_raw = []
+        for z in range(PASSES):
+            t = keep.tile([P, PACK, N], F32, name="w_raw%d" % z, align_bytes=64)
+            nc.sync.dma_start(out=t[:], in_=w_rows[z])
+            w_raw.append(t)
+        for t, src in zip(pos_sb, (pos1, pos2, pos3)):
+            nc.sync.dma_start(t[:], src)
+
+        def s_cast(dst, src):
+            nc.scalar.copy(dst, src)
+
+        warm = keep.tile([P, 2], F32, name="warm")
+        nc.gpsimd.memset(warm[:, 0:1], 0.0)
+        nc.scalar.activation(warm[:, 1:2], warm[:, 0:1], ACT.Gelu_apprx_tanh)
+
+        def cast_pair(q):
+            pairs = keep.tile([P, T, 2], BF16, name="pairs%d" % q, align_bytes=64)
+            for t, c0, cols, on_v in raw[q]:
+                src = t[:].rearrange("p e t -> p t e")
+                on_s = cols - on_v
+                if on_s:
+                    s_cast(pairs[:, c0 : c0 + on_s, :], src[:, :on_s, :])
+                if on_v:
+                    nc.vector.tensor_copy(pairs[:, c0 + on_s : c0 + cols, :], src[:, on_s:, :])
+            return pairs[:].rearrange("p t e -> p (t e)").bitcast(U32)
+
+        def gather(window, picked, u, j0, n):
+            words = picked[:].bitcast(U32).rearrange("p (n u) -> p n u", u=2)
+            nc.vector.tensor_copy(words[:, :, u], window.indirect(offs_sb[:, j0 // 16 : (j0 + n) // 16]))
+
+        def quantize(src, n, name):
+            codes = keep.tile([P, n], U32, name="codes_" + name, align_bytes=64)
+            scales = keep.tile([P, n], U8, name="scales_" + name, align_bytes=64)
+            nc.vector.quantize_mx(out=codes[:].bitcast(FP8X4), scales=scales[:], in_=src)
+            return codes, scales
+
+        picked0 = keep.tile([P, S * PACK], BF16, name="picked0", align_bytes=64)
+        for u in range(2):
+            gather(cast_pair(u), picked0, u, 0, S)
+        x0_codes, x0_scales = quantize(picked0[:], S, "x0")
+
+        starts = [sum(PIECES[:i]) for i in range(len(PIECES))]
+        picked1 = [keep.tile([P, n * PACK], BF16, name="picked1_%d" % i, align_bytes=64) for i, n in enumerate(PIECES)]
+        window = cast_pair(2)
+        for t, j0, n in zip(picked1, starts, PIECES):
+            gather(window, t, 0, j0, n)
+        window = cast_pair(3)
+        w_bf = []
+        for z in range(PASSES):
+            t = keep.tile([P, N, PACK], BF16, name="w_bf%d" % z, align_bytes=64)
+            s_cast(t[:], w_raw[z][:].rearrange("p j m -> p m j"))
+            w_bf.append(t)
+        for t, j0, n in zip(picked1, starts, PIECES):
+            gather(window, t, 1, j0, n)
+        wq = [quantize(w_bf[z][:].rearrange("p m j -> p (m j)"), N, "w%d" % z) for z in range(PASSES)]
+
+        y = keep.tile([P, S], F32, name="y", align_bytes=64)
+        for i, (t, j0, n) in enumerate(zip(picked1, starts, PIECES)):
+            x1_codes, x1_scales = quantize(t[:], n, "x1_%d" % i)
+            acc = psum.tile([P, n], F32, name="acc%d" % i)
+            nc.tensor.matmul_mx(out=acc[:], lhsT=wq[0][0][:].bitcast(FP8X4), lhsT_scale=wq[0][1][:],
+                                rhs=x0_codes[:, j0 : j0 + n].bitcast(FP8X4), rhs_scale=x0_scales[:, j0 : j0 + n],
+                                start=True, stop=False)
+            nc.tensor.matmul_mx(out=acc[:], lhsT=wq[1][0][:].bitcast(FP8X4), lhsT_scale=wq[1][1][:],
+                                rhs=x1_codes[:].bitcast(FP8X4), rhs_scale=x1_scales[:],
+                                start=False, stop=True)
+            nc.scalar.activation(y[:, j0 : j0 + n], acc[:], ACT.Gelu_apprx_tanh)
+
+        nb = [keep.tile([P, V], F32, name="nb%d" % i, align_bytes=64) for i in range(3)]
+        for t, pos in zip(nb, pos_sb):
+            nc.vector.tensor_copy(t[:], y[:].indirect(pos[:]))
+        hi = keep.tile([P, V], F32, name="hi")
+        lo = keep.tile([P, V], F32, name="lo")
+        mid = keep.tile([P, V], F32, name="mid")
+        med = keep.tile([P, V], F32, name="med")
+        halves = [slice(0, V // 2), slice(V // 2, V)]
+        for h in halves:
+            nc.vector.tensor_tensor(hi[:, h], nb[0][:, h], nb[1][:, h], ALU.max)
+            nc.vector.tensor_tensor(lo[:, h], nb[0][:, h], nb[1][:, h], ALU.min)
+        for h in halves:
+            nc.vector.tensor_tensor(mid[:, h], hi[:, h], nb[2][:, h], ALU.min)
+        for h in halves:
+            nc.vector.tensor_tensor(med[:, h], lo[:, h], mid[:, h], ALU.max)
+            nc.sync.dma_start(out=out[:, h], in_=med[:, h])

@@ -8,6 +8,7 @@ FLOPS = 2 * K * N * S
 F32 = mybir.dt.float32
 BF16 = mybir.dt.bfloat16
 U32 = mybir.dt.uint32
+I32 = mybir.dt.int32
 U16 = mybir.dt.uint16
 U8 = mybir.dt.uint8
 FP8X4 = mybir.dt.float8_e4m3fn_x4
@@ -18,8 +19,9 @@ P = 128
 PACK = 4
 K_PASS = P * PACK
 PASSES = K // K_PASS
-CHUNKS = (((512, 512), (512, 320)), ((512, 0), (512, 256)), ((512, 0), (512, 128)), ((512, 0), (256, 0), (256, 160)))
-PIECES = (256, 128, 128)
+CHUNKS = (((512, 0), (512, 320)), ((512, 0), (512, 320)), ((512, 0), (512, 192)), ((512, 0), (256, 128), (256, 192)))
+PIECES = (128, 128, 128, 128)
+WEAVE_ON_VECTOR = (False, False, False, False)
 
 
 def tile_picked_median_gelu_e_kernel(tc, xT, w1, offs, pos1, pos2, pos3, out):
@@ -31,8 +33,9 @@ def tile_picked_median_gelu_e_kernel(tc, xT, w1, offs, pos1, pos2, pos3, out):
         offs_sb = keep.tile([P, S // 16], U16, name="offs_sb")
         pos_sb = [keep.tile([P, V // 16], U16, name="pos_sb%d" % i) for i in range(3)]
         x_rows = xT.rearrange("(z p j) t -> z p j t", p=P, j=PACK)
-        w_rows = w1.rearrange("(z p j) m -> z p j m", p=P, j=PACK)
 
+        w_rows = w1.rearrange("(z p j) m -> z p j m", p=P, j=PACK)
+        w_raw = [keep.tile([P, PACK, N], F32, name="w_raw%d" % z, align_bytes=64) for z in range(PASSES)]
         raw = []
         for q in range(4):
             z, u = divmod(q, 2)
@@ -46,16 +49,10 @@ def tile_picked_median_gelu_e_kernel(tc, xT, w1, offs, pos1, pos2, pos3, out):
                 row.append((t, c0, cols, on_v))
                 c0 = c0 + cols
             raw.append(row)
-        w_raw = []
-        for z in range(PASSES):
-            t = keep.tile([P, PACK, N], F32, name="w_raw%d" % z, align_bytes=64)
-            nc.sync.dma_start(out=t[:], in_=w_rows[z])
-            w_raw.append(t)
+            if q % 2 == 1:
+                nc.sync.dma_start(out=w_raw[z][:], in_=w_rows[z])
         for t, src in zip(pos_sb, (pos1, pos2, pos3)):
             nc.sync.dma_start(t[:], src)
-
-        def s_cast(dst, src):
-            nc.scalar.copy(dst, src)
 
         warm = keep.tile([P, 2], F32, name="warm")
         nc.gpsimd.memset(warm[:, 0:1], 0.0)
@@ -67,14 +64,23 @@ def tile_picked_median_gelu_e_kernel(tc, xT, w1, offs, pos1, pos2, pos3, out):
                 src = t[:].rearrange("p e t -> p t e")
                 on_s = cols - on_v
                 if on_s:
-                    s_cast(pairs[:, c0 : c0 + on_s, :], src[:, :on_s, :])
+                    nc.scalar.copy(pairs[:, c0 : c0 + on_s, :], src[:, :on_s, :])
                 if on_v:
                     nc.vector.tensor_copy(pairs[:, c0 + on_s : c0 + cols, :], src[:, on_s:, :])
             return pairs[:].rearrange("p t e -> p (t e)").bitcast(U32)
 
         def gather(window, picked, u, j0, n):
-            words = picked[:].bitcast(U32).rearrange("p (n u) -> p n u", u=2)
-            nc.vector.tensor_copy(words[:, :, u], window.indirect(offs_sb[:, j0 // 16 : (j0 + n) // 16]))
+            nc.vector.tensor_copy(picked[:, u, :], window.indirect(offs_sb[:, j0 // 16 : (j0 + n) // 16]))
+
+        def weave(picked, n, name, on_vector):
+            woven = keep.tile([P, n * PACK], BF16, name="woven_" + name, align_bytes=64)
+            src = picked[:].rearrange("p u n -> p n u")
+            if on_vector:
+                nc.vector.tensor_copy(woven[:].bitcast(I32).rearrange("p (n u) -> p n u", u=2),
+                                      picked[:].bitcast(I32).rearrange("p u n -> p n u"))
+            else:
+                nc.scalar.copy(woven[:].bitcast(U32).rearrange("p (n u) -> p n u", u=2), src)
+            return woven
 
         def quantize(src, n, name):
             codes = keep.tile([P, n], U32, name="codes_" + name, align_bytes=64)
@@ -82,37 +88,45 @@ def tile_picked_median_gelu_e_kernel(tc, xT, w1, offs, pos1, pos2, pos3, out):
             nc.vector.quantize_mx(out=codes[:].bitcast(FP8X4), scales=scales[:], in_=src)
             return codes, scales
 
-        picked0 = keep.tile([P, S * PACK], BF16, name="picked0", align_bytes=64)
+        def cast_w(z):
+            t = keep.tile([P, N, PACK], BF16, name="w_bf%d" % z, align_bytes=64)
+            nc.scalar.copy(t[:], w_raw[z][:].rearrange("p j m -> p m j"))
+            return t[:].rearrange("p m j -> p (m j)")
+
+        H = S // 2
+        picked0 = [keep.tile([P, 2, H], U32, name="picked0_%d" % h, align_bytes=64) for h in range(2)]
         for u in range(2):
-            gather(cast_pair(u), picked0, u, 0, S)
-        x0_codes, x0_scales = quantize(picked0[:], S, "x0")
+            window = cast_pair(u)
+            for h in range(2):
+                gather(window, picked0[h], u, h * H, H)
+        w_bf0 = cast_w(0)
+        woven0 = [weave(picked0[h], H, "x0_%d" % h, True) for h in range(2)]
+        x0 = [quantize(woven0[h][:], H, "x0_%d" % h) for h in range(2)]
+        w0 = quantize(w_bf0, N, "w0")
 
         starts = [sum(PIECES[:i]) for i in range(len(PIECES))]
-        picked1 = [keep.tile([P, n * PACK], BF16, name="picked1_%d" % i, align_bytes=64) for i, n in enumerate(PIECES)]
-        window = cast_pair(2)
-        for t, j0, n in zip(picked1, starts, PIECES):
-            gather(window, t, 0, j0, n)
-        window = cast_pair(3)
-        w_bf = []
-        for z in range(PASSES):
-            t = keep.tile([P, N, PACK], BF16, name="w_bf%d" % z, align_bytes=64)
-            s_cast(t[:], w_raw[z][:].rearrange("p j m -> p m j"))
-            w_bf.append(t)
-        for t, j0, n in zip(picked1, starts, PIECES):
-            gather(window, t, 1, j0, n)
-        wq = [quantize(w_bf[z][:].rearrange("p m j -> p (m j)"), N, "w%d" % z) for z in range(PASSES)]
+        acc = [psum.tile([P, n], F32, name="acc%d" % i) for i, n in enumerate(PIECES)]
+        for a, j0, n in zip(acc, starts, PIECES):
+            h, c = divmod(j0, H)
+            nc.tensor.matmul_mx(out=a[:], lhsT=w0[0][:].bitcast(FP8X4), lhsT_scale=w0[1][:],
+                                rhs=x0[h][0][:, c : c + n].bitcast(FP8X4), rhs_scale=x0[h][1][:, c : c + n],
+                                start=True, stop=False)
+        picked1 = [keep.tile([P, 2, n], U32, name="picked1_%d" % i, align_bytes=64) for i, n in enumerate(PIECES)]
+        for u in range(2):
+            window = cast_pair(2 + u)
+            for t, j0, n in zip(picked1, starts, PIECES):
+                gather(window, t, u, j0, n)
+        w1q = quantize(cast_w(1), N, "w1")
+        woven1 = [weave(t, n, "x1_%d" % i, WEAVE_ON_VECTOR[i]) for i, (t, n) in enumerate(zip(picked1, PIECES))]
 
         y = keep.tile([P, S], F32, name="y", align_bytes=64)
-        for i, (t, j0, n) in enumerate(zip(picked1, starts, PIECES)):
-            x1_codes, x1_scales = quantize(t[:], n, "x1_%d" % i)
-            acc = psum.tile([P, n], F32, name="acc%d" % i)
-            nc.tensor.matmul_mx(out=acc[:], lhsT=wq[0][0][:].bitcast(FP8X4), lhsT_scale=wq[0][1][:],
-                                rhs=x0_codes[:, j0 : j0 + n].bitcast(FP8X4), rhs_scale=x0_scales[:, j0 : j0 + n],
-                                start=True, stop=False)
-            nc.tensor.matmul_mx(out=acc[:], lhsT=wq[1][0][:].bitcast(FP8X4), lhsT_scale=wq[1][1][:],
+        for i, (j0, n) in enumerate(zip(starts, PIECES)):
+            x1_codes, x1_scales = quantize(woven1[i][:], n, "x1_%d" % i)
+            nc.tensor.matmul_mx(out=acc[i][:], lhsT=w1q[0][:].bitcast(FP8X4), lhsT_scale=w1q[1][:],
                                 rhs=x1_codes[:].bitcast(FP8X4), rhs_scale=x1_scales[:],
                                 start=False, stop=True)
-            nc.scalar.activation(y[:, j0 : j0 + n], acc[:], ACT.Gelu_apprx_tanh)
+        for i, (j0, n) in enumerate(zip(starts, PIECES)):
+            nc.scalar.activation(y[:, j0 : j0 + n], acc[i][:], ACT.Gelu_apprx_tanh)
 
         nb = [keep.tile([P, V], F32, name="nb%d" % i, align_bytes=64) for i in range(3)]
         for t, pos in zip(nb, pos_sb):

@@ -19,7 +19,7 @@ P = 128
 PACK = 4
 K_PASS = P * PACK
 PASSES = K // K_PASS
-CHUNKS = (((512, 0), (512, 320)), ((512, 0), (512, 320)), ((512, 0), (512, 192)), ((512, 0), (256, 128), (256, 192)))
+CHUNKS = (((1024, 640),), ((512, 0), (512, 320)), ((512, 0), (512, 192)), ((512, 0), (512, 352)))
 PIECES = (128, 128, 128, 128)
 WEAVE_ON_VECTOR = (False, False, False, False)
 

@@ -19,7 +19,7 @@ P = 128
 PACK = 4
 K_PASS = P * PACK
 PASSES = K // K_PASS
-CHUNKS = (((1024, 640),), ((512, 0), (512, 320)), ((512, 0), (512, 192)), ((512, 0), (512, 352)))
+CHUNKS = (((1024, 640),), ((1024, 640),), ((512, 0), (512, 96)), ((512, 0), (512, 352)))
 PIECES = (128, 128, 128, 128)
 WEAVE_ON_VECTOR = (False, False, False, False)
 
@@ -136,9 +136,8 @@ def tile_picked_median_gelu_e_kernel(tc, xT, w1, offs, pos1, pos2, pos3, out):
         mid = keep.tile([P, V], F32, name="mid")
         med = keep.tile([P, V], F32, name="med")
         halves = [slice(0, V // 2), slice(V // 2, V)]
-        for h in halves:
-            nc.vector.tensor_tensor(hi[:, h], nb[0][:, h], nb[1][:, h], ALU.max)
-            nc.vector.tensor_tensor(lo[:, h], nb[0][:, h], nb[1][:, h], ALU.min)
+        nc.vector.tensor_tensor(hi[:], nb[0][:], nb[1][:], ALU.max)
+        nc.vector.tensor_tensor(lo[:], nb[0][:], nb[1][:], ALU.min)
         for h in halves:
             nc.vector.tensor_tensor(mid[:, h], hi[:, h], nb[2][:, h], ALU.min)
         for h in halves:

@@ -19,7 +19,7 @@ P = 128
 PACK = 4
 K_PASS = P * PACK
 PASSES = K // K_PASS
-CHUNKS = (((1024, 640),), ((1024, 640),), ((512, 0), (512, 96)), ((512, 0), (512, 352)))
+CHUNKS = (((1024, 0, 672),), ((1024, 0, 640),), ((1024, 0, 544),), ((512, 0, 0), (1024, 0, 384)))
 PIECES = (128, 128, 128, 128)
 WEAVE_ON_VECTOR = (False, False, False, False)
 
@@ -32,25 +32,20 @@ def tile_picked_median_gelu_e_kernel(tc, xT, w1, offs, pos1, pos2, pos3, out):
 
         offs_sb = keep.tile([P, S // 16], U16, name="offs_sb")
         pos_sb = [keep.tile([P, V // 16], U16, name="pos_sb%d" % i) for i in range(3)]
-        x_rows = xT.rearrange("(z p j) t -> z p j t", p=P, j=PACK)
-
         w_rows = w1.rearrange("(z p j) m -> z p j m", p=P, j=PACK)
         w_raw = [keep.tile([P, PACK, N], F32, name="w_raw%d" % z, align_bytes=64) for z in range(PASSES)]
-        raw = []
+        x_flat = xT.rearrange("(z p j) t -> z p (j t)", p=P, j=PACK)
+        raw = [keep.tile([P, 2 * T], F32, name="raw%d" % q, align_bytes=64) for q in range(4)]
         for q in range(4):
             z, u = divmod(q, 2)
-            c0 = 0
-            row = []
-            for i, (cols, on_v) in enumerate(CHUNKS[q]):
-                t = keep.tile([P, 2, cols], F32, name="raw%d_%d" % (q, i), align_bytes=64)
-                nc.sync.dma_start(out=t[:], in_=x_rows[z, :, 2 * u : 2 * u + 2, c0 : c0 + cols])
-                if q == 0 and i == 0:
+            done = 0
+            for end, on_g, on_v in CHUNKS[q]:
+                nc.sync.dma_start(out=raw[q][:, done : T + end], in_=x_flat[z, :, 2 * u * T + done : (2 * u + 1) * T + end])
+                if q == 0 and done == 0:
                     nc.sync.dma_start(offs_sb[:], offs)
-                row.append((t, c0, cols, on_v))
-                c0 = c0 + cols
-            raw.append(row)
-            if q % 2 == 1:
-                nc.sync.dma_start(out=w_raw[z][:], in_=w_rows[z])
+                done = T + end
+        for z in range(PASSES):
+            nc.sync.dma_start(out=w_raw[z][:], in_=w_rows[z])
         for t, src in zip(pos_sb, (pos1, pos2, pos3)):
             nc.sync.dma_start(t[:], src)
 
@@ -60,26 +55,30 @@ def tile_picked_median_gelu_e_kernel(tc, xT, w1, offs, pos1, pos2, pos3, out):
 
         def cast_pair(q):
             pairs = keep.tile([P, T, 2], BF16, name="pairs%d" % q, align_bytes=64)
-            for t, c0, cols, on_v in raw[q]:
-                src = t[:].rearrange("p e t -> p t e")
-                on_s = cols - on_v
-                if on_s:
-                    nc.scalar.copy(pairs[:, c0 : c0 + on_s, :], src[:, :on_s, :])
+            src = raw[q][:].rearrange("p (e t) -> p t e", e=2)
+            c0 = 0
+            for end, on_g, on_v in CHUNKS[q]:
+                cut = end - on_v
+                if on_g:
+                    nc.gpsimd.tensor_copy(pairs[:, c0 : c0 + on_g, :], src[:, c0 : c0 + on_g, :])
+                    c0 = c0 + on_g
+                if cut > c0:
+                    nc.scalar.copy(pairs[:, c0:cut, :], src[:, c0:cut, :])
                 if on_v:
-                    nc.vector.tensor_copy(pairs[:, c0 + on_s : c0 + cols, :], src[:, on_s:, :])
+                    nc.vector.tensor_copy(pairs[:, cut:end, :], src[:, cut:end, :])
+                c0 = end
             return pairs[:].rearrange("p t e -> p (t e)").bitcast(U32)
 
         def gather(window, picked, u, j0, n):
-            nc.vector.tensor_copy(picked[:, u, :], window.indirect(offs_sb[:, j0 // 16 : (j0 + n) // 16]))
+            nc.vector.tensor_copy(picked[:, u, j0 : j0 + n], window.indirect(offs_sb[:, j0 // 16 : (j0 + n) // 16]))
 
-        def weave(picked, n, name, on_vector):
-            woven = keep.tile([P, n * PACK], BF16, name="woven_" + name, align_bytes=64)
-            src = picked[:].rearrange("p u n -> p n u")
+        def weave(picked, j0, n, woven, on_vector):
             if on_vector:
-                nc.vector.tensor_copy(woven[:].bitcast(I32).rearrange("p (n u) -> p n u", u=2),
-                                      picked[:].bitcast(I32).rearrange("p u n -> p n u"))
+                nc.vector.tensor_copy(woven.bitcast(I32).rearrange("p (n u) -> p n u", u=2),
+                                      picked[:].bitcast(I32)[:, :, j0 : j0 + n].rearrange("p u n -> p n u"))
             else:
-                nc.scalar.copy(woven[:].bitcast(U32).rearrange("p (n u) -> p n u", u=2), src)
+                nc.scalar.copy(woven.bitcast(U32).rearrange("p (n u) -> p n u", u=2),
+                               picked[:, :, j0 : j0 + n].rearrange("p u n -> p n u"))
             return woven
 
         def quantize(src, n, name):
@@ -88,45 +87,42 @@ def tile_picked_median_gelu_e_kernel(tc, xT, w1, offs, pos1, pos2, pos3, out):
             nc.vector.quantize_mx(out=codes[:].bitcast(FP8X4), scales=scales[:], in_=src)
             return codes, scales
 
-        def cast_w(z):
-            t = keep.tile([P, N, PACK], BF16, name="w_bf%d" % z, align_bytes=64)
-            nc.scalar.copy(t[:], w_raw[z][:].rearrange("p j m -> p m j"))
-            return t[:].rearrange("p m j -> p (m j)")
+        w_bf = keep.tile([P, PASSES, N, PACK], BF16, name="w_bf", align_bytes=64)
+
+        def cast_w(z, copy):
+            copy(w_bf[:, z], w_raw[z][:].rearrange("p j m -> p m j"))
+
+        def product(acc, wq, m0, xq, c, n, first):
+            nc.tensor.matmul_mx(out=acc[:], lhsT=wq[0][:, m0 : m0 + N].bitcast(FP8X4), lhsT_scale=wq[1][:, m0 : m0 + N],
+                                rhs=xq[0][:, c : c + n].bitcast(FP8X4), rhs_scale=xq[1][:, c : c + n],
+                                start=first, stop=not first)
 
         H = S // 2
-        picked0 = [keep.tile([P, 2, H], U32, name="picked0_%d" % h, align_bytes=64) for h in range(2)]
-        for u in range(2):
-            window = cast_pair(u)
-            for h in range(2):
-                gather(window, picked0[h], u, h * H, H)
-        w_bf0 = cast_w(0)
-        woven0 = [weave(picked0[h], H, "x0_%d" % h, True) for h in range(2)]
-        x0 = [quantize(woven0[h][:], H, "x0_%d" % h) for h in range(2)]
-        w0 = quantize(w_bf0, N, "w0")
-
         starts = [sum(PIECES[:i]) for i in range(len(PIECES))]
+        picked0 = keep.tile([P, 2, S], U32, name="picked0", align_bytes=64)
+        picked1 = keep.tile([P, 2, S], U32, name="picked1", align_bytes=64)
+        woven1 = keep.tile([P, S * PACK], BF16, name="woven1", align_bytes=64)
         acc = [psum.tile([P, n], F32, name="acc%d" % i) for i, n in enumerate(PIECES)]
-        for a, j0, n in zip(acc, starts, PIECES):
-            h, c = divmod(j0, H)
-            nc.tensor.matmul_mx(out=a[:], lhsT=w0[0][:].bitcast(FP8X4), lhsT_scale=w0[1][:],
-                                rhs=x0[h][0][:, c : c + n].bitcast(FP8X4), rhs_scale=x0[h][1][:, c : c + n],
-                                start=True, stop=False)
-        picked1 = [keep.tile([P, 2, n], U32, name="picked1_%d" % i, align_bytes=64) for i, n in enumerate(PIECES)]
-        for u in range(2):
-            window = cast_pair(2 + u)
-            for t, j0, n in zip(picked1, starts, PIECES):
-                gather(window, t, u, j0, n)
-        w1q = quantize(cast_w(1), N, "w1")
-        woven1 = [weave(t, n, "x1_%d" % i, WEAVE_ON_VECTOR[i]) for i, (t, n) in enumerate(zip(picked1, PIECES))]
-
         y = keep.tile([P, S], F32, name="y", align_bytes=64)
-        for i, (j0, n) in enumerate(zip(starts, PIECES)):
-            x1_codes, x1_scales = quantize(woven1[i][:], n, "x1_%d" % i)
-            nc.tensor.matmul_mx(out=acc[i][:], lhsT=w1q[0][:].bitcast(FP8X4), lhsT_scale=w1q[1][:],
-                                rhs=x1_codes[:].bitcast(FP8X4), rhs_scale=x1_scales[:],
-                                start=False, stop=True)
-        for i, (j0, n) in enumerate(zip(starts, PIECES)):
-            nc.scalar.activation(y[:, j0 : j0 + n], acc[i][:], ACT.Gelu_apprx_tanh)
+        gather(cast_pair(0), picked0, 0, 0, S)
+        gather(cast_pair(1), picked0, 1, 0, S)
+        gather(cast_pair(2), picked1, 0, 0, S)
+        woven0 = [weave(picked0, h * H, H, raw[2][:, h * T : h * T + 2 * H].bitcast(BF16), False) for h in range(2)]
+        window = cast_pair(3)
+        x0 = [quantize(woven0[h], H, "x0_%d" % h) for h in range(2)]
+        for j0 in range(0, S, 128):
+            gather(window, picked1, 1, j0, 128)
+        for z in range(PASSES):
+            cast_w(z, nc.scalar.copy)
+        for i, j0 in enumerate(range(0, S, 128)):
+            weave(picked1, j0, 128, woven1[:, j0 * PACK : (j0 + 128) * PACK], WEAVE_ON_VECTOR[i])
+        wq = [quantize(w_bf[:, z].rearrange("p m j -> p (m j)"), N, "w%d" % z) for z in range(PASSES)]
+        for a, j0, n in zip(acc, starts, PIECES):
+            product(a, wq[0], 0, x0[j0 // H], j0 % H, n, True)
+        for a, j0, n in zip(acc, starts, PIECES):
+            product(a, wq[1], 0, quantize(woven1[:, j0 * PACK : (j0 + n) * PACK], n, "x1_%d" % j0), 0, n, False)
+        for a, j0, n in zip(acc, starts, PIECES):
+            nc.scalar.activation(y[:, j0 : j0 + n], a[:], ACT.Gelu_apprx_tanh)
 
         nb = [keep.tile([P, V], F32, name="nb%d" % i, align_bytes=64) for i in range(3)]
         for t, pos in zip(nb, pos_sb):

@@ -19,7 +19,8 @@ P = 128
 PACK = 4
 K_PASS = P * PACK
 PASSES = K // K_PASS
-CHUNKS = (((1024, 0, 672),), ((1024, 0, 640),), ((1024, 0, 544),), ((512, 0, 0), (1024, 0, 384)))
+PAD = 256
+CHUNKS = (((1024, (672,)),), ((1024, (672,)),), ((1024, (336, 672)),), ((512, ()), (1024, (848,))))
 PIECES = (128, 128, 128, 128)
 WEAVE_ON_VECTOR = (False, False, False, False)
 
@@ -35,11 +36,13 @@ def tile_picked_median_gelu_e_kernel(tc, xT, w1, offs, pos1, pos2, pos3, out):
         w_rows = w1.rearrange("(z p j) m -> z p j m", p=P, j=PACK)
         w_raw = [keep.tile([P, PACK, N], F32, name="w_raw%d" % z, align_bytes=64) for z in range(PASSES)]
         x_flat = xT.rearrange("(z p j) t -> z p (j t)", p=P, j=PACK)
-        raw = [keep.tile([P, 2 * T], F32, name="raw%d" % q, align_bytes=64) for q in range(4)]
+        padded = keep.tile([P, PAD + 2 * T + PAD], F32, name="padded", align_bytes=64)
+        raw = [padded[:, PAD : PAD + 2 * T] if q == 2 else keep.tile([P, 2 * T], F32, name="raw%d" % q, align_bytes=64)[:]
+               for q in range(4)]
         for q in range(4):
             z, u = divmod(q, 2)
             done = 0
-            for end, on_g, on_v in CHUNKS[q]:
+            for end, cuts in CHUNKS[q]:
                 nc.sync.dma_start(out=raw[q][:, done : T + end], in_=x_flat[z, :, 2 * u * T + done : (2 * u + 1) * T + end])
                 if q == 0 and done == 0:
                     nc.sync.dma_start(offs_sb[:], offs)
@@ -55,17 +58,13 @@ def tile_picked_median_gelu_e_kernel(tc, xT, w1, offs, pos1, pos2, pos3, out):
 
         def cast_pair(q):
             pairs = keep.tile([P, T, 2], BF16, name="pairs%d" % q, align_bytes=64)
-            src = raw[q][:].rearrange("p (e t) -> p t e", e=2)
+            src = raw[q].rearrange("p (e t) -> p t e", e=2)
             c0 = 0
-            for end, on_g, on_v in CHUNKS[q]:
-                cut = end - on_v
-                if on_g:
-                    nc.gpsimd.tensor_copy(pairs[:, c0 : c0 + on_g, :], src[:, c0 : c0 + on_g, :])
-                    c0 = c0 + on_g
-                if cut > c0:
-                    nc.scalar.copy(pairs[:, c0:cut, :], src[:, c0:cut, :])
-                if on_v:
-                    nc.vector.tensor_copy(pairs[:, cut:end, :], src[:, cut:end, :])
+            for end, cuts in CHUNKS[q]:
+                for c1 in cuts:
+                    nc.vector.tensor_copy(pairs[:, c0:c1, :], src[:, c0:c1, :])
+                    c0 = c1
+                nc.scalar.copy(pairs[:, c0:end, :], src[:, c0:end, :])
                 c0 = end
             return pairs[:].rearrange("p t e -> p (t e)").bitcast(U32)
 
@@ -106,19 +105,24 @@ def tile_picked_median_gelu_e_kernel(tc, xT, w1, offs, pos1, pos2, pos3, out):
         y = keep.tile([P, S], F32, name="y", align_bytes=64)
         gather(cast_pair(0), picked0, 0, 0, S)
         gather(cast_pair(1), picked0, 1, 0, S)
-        gather(cast_pair(2), picked1, 0, 0, S)
-        woven0 = [weave(picked0, h * H, H, raw[2][:, h * T : h * T + 2 * H].bitcast(BF16), False) for h in range(2)]
-        window = cast_pair(3)
+        window = cast_pair(2)
+        woven0 = [padded[:, : 2 * PAD].bitcast(BF16), padded[:, 2 * T :].bitcast(BF16)]
+        weave(picked0, 0, H, woven0[0], True)
+        gather(window, picked1, 0, 0, S)
+        weave(picked0, H, H, woven0[1], False)
         x0 = [quantize(woven0[h], H, "x0_%d" % h) for h in range(2)]
-        for j0 in range(0, S, 128):
+        window = cast_pair(3)
+        cast_w(0, nc.vector.tensor_copy)
+        gather(window, picked1, 1, 0, 128)
+        wq = [quantize(w_bf[:, 0].rearrange("p m j -> p (m j)"), N, "w0")]
+        for j0 in range(128, S, 128):
             gather(window, picked1, 1, j0, 128)
-        for z in range(PASSES):
-            cast_w(z, nc.scalar.copy)
-        for i, j0 in enumerate(range(0, S, 128)):
-            weave(picked1, j0, 128, woven1[:, j0 * PACK : (j0 + 128) * PACK], WEAVE_ON_VECTOR[i])
-        wq = [quantize(w_bf[:, z].rearrange("p m j -> p (m j)"), N, "w%d" % z) for z in range(PASSES)]
         for a, j0, n in zip(acc, starts, PIECES):
             product(a, wq[0], 0, x0[j0 // H], j0 % H, n, True)
+        cast_w(1, nc.scalar.copy)
+        for i, j0 in enumerate(range(0, S, 128)):
+            weave(picked1, j0, 128, woven1[:, j0 * PACK : (j0 + 128) * PACK], WEAVE_ON_VECTOR[i])
+        wq.append(quantize(w_bf[:, 1].rearrange("p m j -> p (m j)"), N, "w1"))
         for a, j0, n in zip(acc, starts, PIECES):
             product(a, wq[1], 0, quantize(woven1[:, j0 * PACK : (j0 + n) * PACK], n, "x1_%d" % j0), 0, n, False)
         for a, j0, n in zip(acc, starts, PIECES):

@@ -19,10 +19,9 @@ P = 128
 PACK = 4
 K_PASS = P * PACK
 PASSES = K // K_PASS
-PAD = 256
-CHUNKS = (((1024, (672,)),), ((1024, (672,)),), ((1024, (336, 672)),), ((512, ()), (1024, (848,))))
+PAD = 384
+CHUNKS = (((1024, (672,)),), ((1024, (672,)),), ((512, ()), (512, (168, 336))), ((512, ()), (512, (336,))))
 PIECES = (128, 128, 128, 128)
-WEAVE_ON_VECTOR = (False, False, False, False)
 
 
 def tile_picked_median_gelu_e_kernel(tc, xT, w1, offs, pos1, pos2, pos3, out):
@@ -34,21 +33,29 @@ def tile_picked_median_gelu_e_kernel(tc, xT, w1, offs, pos1, pos2, pos3, out):
         offs_sb = keep.tile([P, S // 16], U16, name="offs_sb")
         pos_sb = [keep.tile([P, V // 16], U16, name="pos_sb%d" % i) for i in range(3)]
         w_rows = w1.rearrange("(z p j) m -> z p j m", p=P, j=PACK)
-        w_raw = [keep.tile([P, PACK, N], F32, name="w_raw%d" % z, align_bytes=64) for z in range(PASSES)]
-        x_flat = xT.rearrange("(z p j) t -> z p (j t)", p=P, j=PACK)
-        padded = keep.tile([P, PAD + 2 * T + PAD], F32, name="padded", align_bytes=64)
-        raw = [padded[:, PAD : PAD + 2 * T] if q == 2 else keep.tile([P, 2 * T], F32, name="raw%d" % q, align_bytes=64)[:]
-               for q in range(4)]
+        shared = keep.tile([P, 2 * S - 128 + PACK * N], F32, name="shared", align_bytes=64)
+        w_raw = [shared[:, 2 * S - 128 :].rearrange("p (j m) -> p j m", j=PACK),
+                 keep.tile([P, PACK, N], F32, name="w_raw1", align_bytes=64)[:]]
+        x_rows = xT.rearrange("(z p j) t -> z p j t", p=P, j=PACK)
+        padded = keep.tile([P, PAD + T + PAD], F32, name="padded", align_bytes=64)
+        raw = []
         for q in range(4):
             z, u = divmod(q, 2)
-            done = 0
-            for end, cuts in CHUNKS[q]:
-                nc.sync.dma_start(out=raw[q][:, done : T + end], in_=x_flat[z, :, 2 * u * T + done : (2 * u + 1) * T + end])
-                if q == 0 and done == 0:
+            c0 = 0
+            row = []
+            for i, (cols, cuts) in enumerate(CHUNKS[q]):
+                if (q, i) == (2, 1):
+                    t = padded[:, PAD : PAD + T].rearrange("p (e t) -> p e t", e=2)
+                else:
+                    t = keep.tile([P, 2, cols], F32, name="raw%d_%d" % (q, i), tag="raw%d_%d" % (q, i), align_bytes=64)[:]
+                nc.sync.dma_start(out=t, in_=x_rows[z, :, 2 * u : 2 * u + 2, c0 : c0 + cols])
+                if q == 0 and i == 0:
                     nc.sync.dma_start(offs_sb[:], offs)
-                done = T + end
+                row.append((t.rearrange("p e t -> p t e"), c0, cols, cuts))
+                c0 = c0 + cols
+            raw.append(row)
         for z in range(PASSES):
-            nc.sync.dma_start(out=w_raw[z][:], in_=w_rows[z])
+            nc.sync.dma_start(out=w_raw[z], in_=w_rows[z])
         for t, src in zip(pos_sb, (pos1, pos2, pos3)):
             nc.sync.dma_start(t[:], src)
 
@@ -58,14 +65,12 @@ def tile_picked_median_gelu_e_kernel(tc, xT, w1, offs, pos1, pos2, pos3, out):
 
         def cast_pair(q):
             pairs = keep.tile([P, T, 2], BF16, name="pairs%d" % q, align_bytes=64)
-            src = raw[q].rearrange("p (e t) -> p t e", e=2)
-            c0 = 0
-            for end, cuts in CHUNKS[q]:
-                for c1 in cuts:
-                    nc.vector.tensor_copy(pairs[:, c0:c1, :], src[:, c0:c1, :])
-                    c0 = c1
-                nc.scalar.copy(pairs[:, c0:end, :], src[:, c0:end, :])
-                c0 = end
+            for src, c0, cols, cuts in raw[q]:
+                done = 0
+                for cut in cuts:
+                    nc.vector.tensor_copy(pairs[:, c0 + done : c0 + cut, :], src[:, done:cut, :])
+                    done = cut
+                nc.scalar.copy(pairs[:, c0 + done : c0 + cols, :], src[:, done:, :])
             return pairs[:].rearrange("p t e -> p (t e)").bitcast(U32)
 
         def gather(window, picked, u, j0, n):
@@ -74,14 +79,14 @@ def tile_picked_median_gelu_e_kernel(tc, xT, w1, offs, pos1, pos2, pos3, out):
         def weave(picked, j0, n, woven, on_vector):
             if on_vector:
                 nc.vector.tensor_copy(woven.bitcast(I32).rearrange("p (n u) -> p n u", u=2),
-                                      picked[:].bitcast(I32)[:, :, j0 : j0 + n].rearrange("p u n -> p n u"))
+                                      picked.bitcast(I32)[:, :, j0 : j0 + n].rearrange("p u n -> p n u"))
             else:
                 nc.scalar.copy(woven.bitcast(U32).rearrange("p (n u) -> p n u", u=2),
                                picked[:, :, j0 : j0 + n].rearrange("p u n -> p n u"))
             return woven
 
-        def quantize(src, n, name):
-            codes = keep.tile([P, n], U32, name="codes_" + name, align_bytes=64)
+        def quantize(src, n, name, tag=None):
+            codes = keep.tile([P, n], U32, name="codes_" + name, tag=tag or "codes_" + name, align_bytes=64)
             scales = keep.tile([P, n], U8, name="scales_" + name, align_bytes=64)
             nc.vector.quantize_mx(out=codes[:].bitcast(FP8X4), scales=scales[:], in_=src)
             return codes, scales
@@ -89,7 +94,7 @@ def tile_picked_median_gelu_e_kernel(tc, xT, w1, offs, pos1, pos2, pos3, out):
         w_bf = keep.tile([P, PASSES, N, PACK], BF16, name="w_bf", align_bytes=64)
 
         def cast_w(z, copy):
-            copy(w_bf[:, z], w_raw[z][:].rearrange("p j m -> p m j"))
+            copy(w_bf[:, z], w_raw[z].rearrange("p j m -> p m j"))
 
         def product(acc, wq, m0, xq, c, n, first):
             nc.tensor.matmul_mx(out=acc[:], lhsT=wq[0][:, m0 : m0 + N].bitcast(FP8X4), lhsT_scale=wq[1][:, m0 : m0 + N],
@@ -98,30 +103,32 @@ def tile_picked_median_gelu_e_kernel(tc, xT, w1, offs, pos1, pos2, pos3, out):
 
         H = S // 2
         starts = [sum(PIECES[:i]) for i in range(len(PIECES))]
-        picked0 = keep.tile([P, 2, S], U32, name="picked0", align_bytes=64)
-        picked1 = keep.tile([P, 2, S], U32, name="picked1", align_bytes=64)
+        picked0 = keep.tile([P, 2, S], U32, name="picked0", align_bytes=64)[:]
+        picked1 = shared[:, : 2 * S].bitcast(U32).rearrange("p (u n) -> p u n", u=2)
         woven1 = keep.tile([P, S * PACK], BF16, name="woven1", align_bytes=64)
         acc = [psum.tile([P, n], F32, name="acc%d" % i) for i, n in enumerate(PIECES)]
         y = keep.tile([P, S], F32, name="y", align_bytes=64)
         gather(cast_pair(0), picked0, 0, 0, S)
         gather(cast_pair(1), picked0, 1, 0, S)
         window = cast_pair(2)
-        woven0 = [padded[:, : 2 * PAD].bitcast(BF16), padded[:, 2 * T :].bitcast(BF16)]
+        woven0 = [padded[:, : 2 * H].bitcast(BF16), padded[:, 2 * PAD + T - 2 * H :].bitcast(BF16)]
         weave(picked0, 0, H, woven0[0], True)
         gather(window, picked1, 0, 0, S)
         weave(picked0, H, H, woven0[1], False)
-        x0 = [quantize(woven0[h], H, "x0_%d" % h) for h in range(2)]
+        x0 = [quantize(woven0[0], H, "x0_0")]
         window = cast_pair(3)
-        cast_w(0, nc.vector.tensor_copy)
-        gather(window, picked1, 1, 0, 128)
-        wq = [quantize(w_bf[:, 0].rearrange("p m j -> p (m j)"), N, "w0")]
-        for j0 in range(128, S, 128):
+        x0.append(quantize(woven0[1], H, "x0_1", "raw3_0"))
+        cast_w(0, nc.scalar.copy)
+        for j0 in range(0, S - 128, 128):
             gather(window, picked1, 1, j0, 128)
+        wq = [quantize(w_bf[:, 0].rearrange("p m j -> p (m j)"), N, "w0")]
+        gather(window, picked1, 1, S - 128, 128)
         for a, j0, n in zip(acc, starts, PIECES):
             product(a, wq[0], 0, x0[j0 // H], j0 % H, n, True)
-        cast_w(1, nc.scalar.copy)
+        for copy, cols in ((nc.scalar.copy, slice(0, N // 2)), (nc.vector.tensor_copy, slice(N // 2, N))):
+            copy(w_bf[:, 1, cols, :], w_raw[1][:, :, cols].rearrange("p j m -> p m j"))
         for i, j0 in enumerate(range(0, S, 128)):
-            weave(picked1, j0, 128, woven1[:, j0 * PACK : (j0 + 128) * PACK], WEAVE_ON_VECTOR[i])
+            weave(picked1, j0, 128, woven1[:, j0 * PACK : (j0 + 128) * PACK], False)
         wq.append(quantize(w_bf[:, 1].rearrange("p m j -> p (m j)"), N, "w1"))
         for a, j0, n in zip(acc, starts, PIECES):
             product(a, wq[1], 0, quantize(woven1[:, j0 * PACK : (j0 + n) * PACK], n, "x1_%d" % j0), 0, n, False)

@@ -125,7 +125,7 @@ def tile_picked_median_gelu_e_kernel(tc, xT, w1, offs, pos1, pos2, pos3, out):
         gather(window, picked1, 1, S - 128, 128)
         for a, j0, n in zip(acc, starts, PIECES):
             product(a, wq[0], 0, x0[j0 // H], j0 % H, n, True)
-        for copy, cols in ((nc.scalar.copy, slice(0, N // 2)), (nc.vector.tensor_copy, slice(N // 2, N))):
+        for copy, cols in ((nc.scalar.copy, slice(0, 96)), (nc.vector.tensor_copy, slice(96, N))):
             copy(w_bf[:, 1, cols, :], w_raw[1][:, :, cols].rearrange("p j m -> p m j"))
         for i, j0 in enumerate(range(0, S, 128)):
             weave(picked1, j0, 128, woven1[:, j0 * PACK : (j0 + 128) * PACK], False)
@@ -142,7 +142,7 @@ def tile_picked_median_gelu_e_kernel(tc, xT, w1, offs, pos1, pos2, pos3, out):
         lo = keep.tile([P, V], F32, name="lo")
         mid = keep.tile([P, V], F32, name="mid")
         med = keep.tile([P, V], F32, name="med")
-        halves = [slice(0, V // 2), slice(V // 2, V)]
+        halves = [slice(0, 96), slice(96, V)]
         nc.vector.tensor_tensor(hi[:], nb[0][:], nb[1][:], ALU.max)
         nc.vector.tensor_tensor(lo[:], nb[0][:], nb[1][:], ALU.min)
         for h in halves:

@@ -125,7 +125,7 @@ def tile_picked_median_gelu_e_kernel(tc, xT, w1, offs, pos1, pos2, pos3, out):
         gather(window, picked1, 1, S - 128, 128)
         for a, j0, n in zip(acc, starts, PIECES):
             product(a, wq[0], 0, x0[j0 // H], j0 % H, n, True)
-        for copy, cols in ((nc.scalar.copy, slice(0, 96)), (nc.vector.tensor_copy, slice(96, N))):
+        for copy, cols in ((nc.scalar.copy, slice(0, 64)), (nc.gpsimd.tensor_copy, slice(64, N))):
             copy(w_bf[:, 1, cols, :], w_raw[1][:, :, cols].rearrange("p j m -> p m j"))
         for i, j0 in enumerate(range(0, S, 128)):
             weave(picked1, j0, 128, woven1[:, j0 * PACK : (j0 + 128) * PACK], False)

@@ -104,8 +104,9 @@ def tile_picked_median_gelu_e_kernel(tc, xT, w1, offs, pos1, pos2, pos3, out):
         H = S // 2
         starts = [sum(PIECES[:i]) for i in range(len(PIECES))]
         picked0 = keep.tile([P, 2, S], U32, name="picked0", align_bytes=64)[:]
-        picked1 = shared[:, : 2 * S].bitcast(U32).rearrange("p (u n) -> p u n", u=2)
-        woven1 = keep.tile([P, S * PACK], BF16, name="woven1", align_bytes=64)
+        picked1 = shared[:, : 2 * S].bitcast(U32).rearrange("p (i u n) -> p i u n", u=2, n=128)
+        woven1 = keep.tile([P, (S - 128) * PACK], BF16, name="woven1", align_bytes=64)
+        woven1 = [woven1[:, i * 512 : (i + 1) * 512] for i in range(3)] + [shared[:, :256].bitcast(BF16)]
         acc = [psum.tile([P, n], F32, name="acc%d" % i) for i, n in enumerate(PIECES)]
         y = keep.tile([P, S], F32, name="y", align_bytes=64)
         gather(cast_pair(0), picked0, 0, 0, S)
@@ -113,25 +114,27 @@ def tile_picked_median_gelu_e_kernel(tc, xT, w1, offs, pos1, pos2, pos3, out):
         window = cast_pair(2)
         woven0 = [padded[:, : 2 * H].bitcast(BF16), padded[:, 2 * PAD + T - 2 * H :].bitcast(BF16)]
         weave(picked0, 0, H, woven0[0], True)
-        gather(window, picked1, 0, 0, S)
+        nc.vector.tensor_copy(picked1[:, :, 0, :], window.indirect(offs_sb[:]))
         weave(picked0, H, H, woven0[1], False)
         x0 = [quantize(woven0[0], H, "x0_0")]
         window = cast_pair(3)
         x0.append(quantize(woven0[1], H, "x0_1", "raw3_0"))
         cast_w(0, nc.scalar.copy)
-        for j0 in range(0, S - 128, 128):
-            gather(window, picked1, 1, j0, 128)
+        nc.vector.tensor_copy(picked1[:, :2, 1, :], window.indirect(offs_sb[:, :16]))
+        nc.vector.tensor_copy(picked1[:, 2, 1, :], window.indirect(offs_sb[:, 16:24]))
         wq = [quantize(w_bf[:, 0].rearrange("p m j -> p (m j)"), N, "w0")]
-        gather(window, picked1, 1, S - 128, 128)
+        nc.vector.tensor_copy(picked1[:, 3, 1, :], window.indirect(offs_sb[:, 24:]))
         for a, j0, n in zip(acc, starts, PIECES):
             product(a, wq[0], 0, x0[j0 // H], j0 % H, n, True)
         for copy, cols in ((nc.scalar.copy, slice(0, 64)), (nc.gpsimd.tensor_copy, slice(64, N))):
             copy(w_bf[:, 1, cols, :], w_raw[1][:, :, cols].rearrange("p j m -> p m j"))
-        for i, j0 in enumerate(range(0, S, 128)):
-            weave(picked1, j0, 128, woven1[:, j0 * PACK : (j0 + 128) * PACK], False)
+        for i in range(3):
+            weave(picked1[:, i], 0, 128, woven1[i], False)
         wq.append(quantize(w_bf[:, 1].rearrange("p m j -> p (m j)"), N, "w1"))
         for a, j0, n in zip(acc, starts, PIECES):
-            product(a, wq[1], 0, quantize(woven1[:, j0 * PACK : (j0 + n) * PACK], n, "x1_%d" % j0), 0, n, False)
+            product(a, wq[1], 0, quantize(woven1[j0 // 128], n, "x1_%d" % j0), 0, n, False)
+            if j0 == 0:
+                weave(picked1[:, 3], 0, 128, woven1[3], True)
         for a, j0, n in zip(acc, starts, PIECES):
             nc.scalar.activation(y[:, j0 : j0 + n], a[:], ACT.Gelu_apprx_tanh)
 

@@ -20,7 +20,7 @@ PACK = 4
 K_PASS = P * PACK
 PASSES = K // K_PASS
 PAD = 384
-CHUNKS = (((1024, (672,)),), ((1024, (672,)),), ((512, ()), (512, (168, 336))), ((512, ()), (512, (336,))))
+CHUNKS = (((1024, (648,)),), ((1024, (648,)),), ((512, ()), (512, (296,))), ((512, ()), (512, (304,))))
 PIECES = (128, 128, 128, 128)
 
 
@@ -37,7 +37,7 @@ def tile_picked_median_gelu_e_kernel(tc, xT, w1, offs, pos1, pos2, pos3, out):
         w_raw = [shared[:, 2 * S - 128 :].rearrange("p (j m) -> p j m", j=PACK),
                  keep.tile([P, PACK, N], F32, name="w_raw1", align_bytes=64)[:]]
         x_rows = xT.rearrange("(z p j) t -> z p j t", p=P, j=PACK)
-        padded = keep.tile([P, PAD + T + PAD], F32, name="padded", align_bytes=64)
+        padded = keep.tile([P, T], F32, name="padded", align_bytes=64)
         raw = []
         for q in range(4):
             z, u = divmod(q, 2)
@@ -45,7 +45,7 @@ def tile_picked_median_gelu_e_kernel(tc, xT, w1, offs, pos1, pos2, pos3, out):
             row = []
             for i, (cols, cuts) in enumerate(CHUNKS[q]):
                 if (q, i) == (2, 1):
-                    t = padded[:, PAD : PAD + T].rearrange("p (e t) -> p e t", e=2)
+                    t = padded[:].rearrange("p (e t) -> p e t", e=2)
                 else:
                     t = keep.tile([P, 2, cols], F32, name="raw%d_%d" % (q, i), tag="raw%d_%d" % (q, i), align_bytes=64)[:]
                 nc.sync.dma_start(out=t, in_=x_rows[z, :, 2 * u : 2 * u + 2, c0 : c0 + cols])
@@ -110,22 +110,34 @@ def tile_picked_median_gelu_e_kernel(tc, xT, w1, offs, pos1, pos2, pos3, out):
         acc = [psum.tile([P, n], F32, name="acc%d" % i) for i, n in enumerate(PIECES)]
         y = keep.tile([P, S], F32, name="y", align_bytes=64)
         gather(cast_pair(0), picked0, 0, 0, S)
-        gather(cast_pair(1), picked0, 1, 0, S)
+        window = cast_pair(1)
+        gather(window, picked0, 1, 0, 128)
+        gather(window, picked0, 1, 128, 384)
+
+        def weave_gpsimd(j0, n, woven):
+            nc.gpsimd.tensor_copy(woven.bitcast(I32).rearrange("p (n u) -> p n u", u=2),
+                                  picked0.bitcast(I32)[:, :, j0 : j0 + n].rearrange("p u n -> p n u"))
+
+        first = keep.tile([P, 128 * PACK], BF16, name="first", align_bytes=64)[:]
+        weave_gpsimd(0, 128, first)
         window = cast_pair(2)
-        woven0 = [padded[:, : 2 * H].bitcast(BF16), padded[:, 2 * PAD + T - 2 * H :].bitcast(BF16)]
-        weave(picked0, 0, H, woven0[0], True)
+        x0 = [(quantize(first, 128, "x0_0", "raw2_0"), 0)]
         nc.vector.tensor_copy(picked1[:, :, 0, :], window.indirect(offs_sb[:]))
-        weave(picked0, H, H, woven0[1], False)
-        x0 = [quantize(woven0[0], H, "x0_0")]
+        second = padded[:, :256].bitcast(BF16)
+        rest = padded[:, 512:].bitcast(BF16)
+        weave(picked0, 128, 128, second, False)
+        weave_gpsimd(256, 256, rest)
+        x0.append((quantize(second, 128, "x0_1"), 0))
         window = cast_pair(3)
-        x0.append(quantize(woven0[1], H, "x0_1", "raw3_0"))
+        wide = quantize(rest, 256, "x0_2", "raw3_0")
+        x0.extend([(wide, 0), (wide, 128)])
         cast_w(0, nc.scalar.copy)
         nc.vector.tensor_copy(picked1[:, :2, 1, :], window.indirect(offs_sb[:, :16]))
         nc.vector.tensor_copy(picked1[:, 2, 1, :], window.indirect(offs_sb[:, 16:24]))
         wq = [quantize(w_bf[:, 0].rearrange("p m j -> p (m j)"), N, "w0")]
         nc.vector.tensor_copy(picked1[:, 3, 1, :], window.indirect(offs_sb[:, 24:]))
         for a, j0, n in zip(acc, starts, PIECES):
-            product(a, wq[0], 0, x0[j0 // H], j0 % H, n, True)
+            product(a, wq[0], 0, x0[j0 // 128][0], x0[j0 // 128][1], n, True)
         for copy, cols in ((nc.scalar.copy, slice(0, 64)), (nc.gpsimd.tensor_copy, slice(64, N))):
             copy(w_bf[:, 1, cols, :], w_raw[1][:, :, cols].rearrange("p j m -> p m j"))
         for i in range(3):

@@ -8,7 +8,6 @@ FLOPS = 2 * K * N * S
 F32 = mybir.dt.float32
 BF16 = mybir.dt.bfloat16
 U32 = mybir.dt.uint32
-I32 = mybir.dt.int32
 U16 = mybir.dt.uint16
 U8 = mybir.dt.uint8
 FP8X4 = mybir.dt.float8_e4m3fn_x4
@@ -17,11 +16,10 @@ ACT = mybir.ActivationFunctionType
 
 P = 128
 PACK = 4
-K_PASS = P * PACK
-PASSES = K // K_PASS
-PAD = 384
-CHUNKS = (((1024, (648,)),), ((1024, (648,)),), ((512, ()), (512, (296,))), ((512, ()), (512, (304,))))
-PIECES = (128, 128, 128, 128)
+PASSES = K // (P * PACK)
+PIECE = 128
+PIECES = S // PIECE
+SHARES = (224, 224, 160)
 
 
 def tile_picked_median_gelu_e_kernel(tc, xT, w1, offs, pos1, pos2, pos3, out):
@@ -32,30 +30,17 @@ def tile_picked_median_gelu_e_kernel(tc, xT, w1, offs, pos1, pos2, pos3, out):
 
         offs_sb = keep.tile([P, S // 16], U16, name="offs_sb")
         pos_sb = [keep.tile([P, V // 16], U16, name="pos_sb%d" % i) for i in range(3)]
-        w_rows = w1.rearrange("(z p j) m -> z p j m", p=P, j=PACK)
-        shared = keep.tile([P, 2 * S - 128 + PACK * N], F32, name="shared", align_bytes=64)
-        w_raw = [shared[:, 2 * S - 128 :].rearrange("p (j m) -> p j m", j=PACK),
-                 keep.tile([P, PACK, N], F32, name="w_raw1", align_bytes=64)[:]]
-        x_rows = xT.rearrange("(z p j) t -> z p j t", p=P, j=PACK)
-        padded = keep.tile([P, T], F32, name="padded", align_bytes=64)
-        raw = []
-        for q in range(4):
-            z, u = divmod(q, 2)
-            c0 = 0
-            row = []
-            for i, (cols, cuts) in enumerate(CHUNKS[q]):
-                if (q, i) == (2, 1):
-                    t = padded[:].rearrange("p (e t) -> p e t", e=2)
-                else:
-                    t = keep.tile([P, 2, cols], F32, name="raw%d_%d" % (q, i), tag="raw%d_%d" % (q, i), align_bytes=64)[:]
-                nc.sync.dma_start(out=t, in_=x_rows[z, :, 2 * u : 2 * u + 2, c0 : c0 + cols])
-                if q == 0 and i == 0:
-                    nc.sync.dma_start(offs_sb[:], offs)
-                row.append((t.rearrange("p e t -> p t e"), c0, cols, cuts))
-                c0 = c0 + cols
-            raw.append(row)
+        x_rows = xT.rearrange("(z p j) t -> z j p t", p=P, j=PACK)
+        w_rows = w1.rearrange("(z p j) m -> p z j m", p=P, j=PACK)
+        raw = [[keep.tile([P, T], F32, name="raw%d_%d" % (z, j), align_bytes=64) for j in range(PACK)] for z in range(PASSES)]
+        w_raw = keep.tile([P, PASSES, PACK, N], F32, name="w_raw", align_bytes=64)
         for z in range(PASSES):
-            nc.sync.dma_start(out=w_raw[z], in_=w_rows[z])
+            for j in range(PACK):
+                nc.sync.dma_start(out=raw[z][j][:], in_=x_rows[z, j])
+                if (z, j) == (0, 0):
+                    nc.sync.dma_start(offs_sb[:], offs)
+            if z == 0:
+                nc.sync.dma_start(out=w_raw[:], in_=w_rows)
         for t, src in zip(pos_sb, (pos1, pos2, pos3)):
             nc.sync.dma_start(t[:], src)
 
@@ -63,105 +48,87 @@ def tile_picked_median_gelu_e_kernel(tc, xT, w1, offs, pos1, pos2, pos3, out):
         nc.gpsimd.memset(warm[:, 0:1], 0.0)
         nc.scalar.activation(warm[:, 1:2], warm[:, 0:1], ACT.Gelu_apprx_tanh)
 
-        def cast_pair(q):
-            pairs = keep.tile([P, T, 2], BF16, name="pairs%d" % q, align_bytes=64)
-            for src, c0, cols, cuts in raw[q]:
-                done = 0
-                for cut in cuts:
-                    nc.vector.tensor_copy(pairs[:, c0 + done : c0 + cut, :], src[:, done:cut, :])
-                    done = cut
-                nc.scalar.copy(pairs[:, c0 + done : c0 + cols, :], src[:, done:, :])
-            return pairs[:].rearrange("p t e -> p (t e)").bitcast(U32)
+        def gather_v(dst, window, offsets, j0, n):
+            nc.vector.tensor_copy(dst, window[:].indirect(offsets[:, j0 // 16 : (j0 + n) // 16]))
 
-        def gather(window, picked, u, j0, n):
-            nc.vector.tensor_copy(picked[:, u, j0 : j0 + n], window.indirect(offs_sb[:, j0 // 16 : (j0 + n) // 16]))
+        def gather_s(dst, window, offsets, j0, n):
+            nc.scalar.activation(dst, window[:].indirect(offsets[:, j0 // 16 : (j0 + n) // 16]), ACT.Copy)
 
-        def weave(picked, j0, n, woven, on_vector):
-            if on_vector:
-                nc.vector.tensor_copy(woven.bitcast(I32).rearrange("p (n u) -> p n u", u=2),
-                                      picked.bitcast(I32)[:, :, j0 : j0 + n].rearrange("p u n -> p n u"))
-            else:
-                nc.scalar.copy(woven.bitcast(U32).rearrange("p (n u) -> p n u", u=2),
-                               picked[:, :, j0 : j0 + n].rearrange("p u n -> p n u"))
-            return woven
-
-        def quantize(src, n, name, tag=None):
-            codes = keep.tile([P, n], U32, name="codes_" + name, tag=tag or "codes_" + name, align_bytes=64)
+        def quantize(src, n, name):
+            codes = keep.tile([P, n], U32, name="codes_" + name, align_bytes=64)
             scales = keep.tile([P, n], U8, name="scales_" + name, align_bytes=64)
             nc.vector.quantize_mx(out=codes[:].bitcast(FP8X4), scales=scales[:], in_=src)
             return codes, scales
 
+        def product(acc, wq, z, xq, c):
+            nc.tensor.matmul_mx(out=acc[:], lhsT=wq[0][:, z * N : (z + 1) * N].bitcast(FP8X4), lhsT_scale=wq[1][:, z * N : (z + 1) * N],
+                                rhs=xq[0][:, c : c + PIECE].bitcast(FP8X4), rhs_scale=xq[1][:, c : c + PIECE],
+                                start=z == 0, stop=z == PASSES - 1)
+
+        acc = [psum.tile([P, PIECE], F32, name="acc%d" % i) for i in range(PIECES)]
         w_bf = keep.tile([P, PASSES, N, PACK], BF16, name="w_bf", align_bytes=64)
 
-        def cast_w(z, copy):
-            copy(w_bf[:, z], w_raw[z].rearrange("p j m -> p m j"))
+        def front_pair(z, u, woven):
+            share = SHARES[2 * z + u]
+            planes = keep.tile([P, 2, S - share], BF16, name="planes%d_%d" % (z, u), align_bytes=64)
+            for e in range(2):
+                gather_v(woven[:, :share, 2 * u + e], raw[z][2 * u + e], offs_sb, 0, share)
+                gather_s(planes[:, e, :], raw[z][2 * u + e], offs_sb, share, S - share)
+            nc.vector.tensor_copy(woven[:, share:, 2 * u : 2 * u + 2], planes[:].rearrange("p j n -> p n j"))
 
-        def product(acc, wq, m0, xq, c, n, first):
-            nc.tensor.matmul_mx(out=acc[:], lhsT=wq[0][:, m0 : m0 + N].bitcast(FP8X4), lhsT_scale=wq[1][:, m0 : m0 + N],
-                                rhs=xq[0][:, c : c + n].bitcast(FP8X4), rhs_scale=xq[1][:, c : c + n],
-                                start=first, stop=not first)
+        woven0 = keep.tile([P, S, PACK], BF16, name="woven0", align_bytes=64)
+        front_pair(0, 0, woven0)
+        front_pair(0, 1, woven0)
+        x0 = quantize(woven0[:].rearrange("p n j -> p (n j)"), S, "x0")
+        nc.scalar.copy(w_bf[:, 0], w_raw[:, 0].rearrange("p j m -> p m j"))
+        nc.vector.tensor_copy(w_bf[:, 1], w_raw[:, 1].rearrange("p j m -> p m j"))
+        wq = quantize(w_bf[:].rearrange("p z m j -> p (z m j)"), PASSES * N, "w")
+        for i in range(PIECES):
+            product(acc[i], wq, 0, x0, i * PIECE)
 
-        H = S // 2
-        starts = [sum(PIECES[:i]) for i in range(len(PIECES))]
-        picked0 = keep.tile([P, 2, S], U32, name="picked0", align_bytes=64)[:]
-        picked1 = shared[:, : 2 * S].bitcast(U32).rearrange("p (i u n) -> p i u n", u=2, n=128)
-        woven1 = keep.tile([P, (S - 128) * PACK], BF16, name="woven1", align_bytes=64)
-        woven1 = [woven1[:, i * 512 : (i + 1) * 512] for i in range(3)] + [shared[:, :256].bitcast(BF16)]
-        acc = [psum.tile([P, n], F32, name="acc%d" % i) for i, n in enumerate(PIECES)]
+        woven1 = keep.tile([P, S, PACK], BF16, name="woven1", align_bytes=64)
+        front_pair(1, 0, woven1)
+        back = keep.tile([P, PIECES - 1, 2, PIECE], BF16, name="back", align_bytes=64)
+        for e in range(2):
+            gather_v(woven1[:, :PIECE, 2 + e], raw[1][2 + e], offs_sb, 0, PIECE)
+            for i in range(1, PIECES):
+                gather_s(back[:, i - 1, e, :], raw[1][2 + e], offs_sb, i * PIECE, PIECE)
+
+        def place(i, copy):
+            copy(woven1[:, i * PIECE : (i + 1) * PIECE, 2:4], back[:, i - 1].rearrange("p j n -> p n j"))
+
+        def quantize_piece(i):
+            return quantize(woven1[:, i * PIECE : (i + 1) * PIECE, :].rearrange("p n j -> p (n j)"), PIECE, "x1_%d" % i)
+
+        place(1, nc.vector.tensor_copy)
+        x1 = [quantize_piece(0)]
+        place(2, nc.vector.tensor_copy)
+        x1.append(quantize_piece(1))
+        place(3, nc.vector.tensor_copy)
+        x1.extend(quantize_piece(i) for i in range(2, PIECES))
         y = keep.tile([P, S], F32, name="y", align_bytes=64)
-        gather(cast_pair(0), picked0, 0, 0, S)
-        window = cast_pair(1)
-        gather(window, picked0, 1, 0, 128)
-        gather(window, picked0, 1, 128, 384)
-
-        def weave_gpsimd(j0, n, woven):
-            nc.gpsimd.tensor_copy(woven.bitcast(I32).rearrange("p (n u) -> p n u", u=2),
-                                  picked0.bitcast(I32)[:, :, j0 : j0 + n].rearrange("p u n -> p n u"))
-
-        first = keep.tile([P, 128 * PACK], BF16, name="first", align_bytes=64)[:]
-        weave_gpsimd(0, 128, first)
-        window = cast_pair(2)
-        x0 = [(quantize(first, 128, "x0_0", "raw2_0"), 0)]
-        nc.vector.tensor_copy(picked1[:, :, 0, :], window.indirect(offs_sb[:]))
-        second = padded[:, :256].bitcast(BF16)
-        rest = padded[:, 512:].bitcast(BF16)
-        weave(picked0, 128, 128, second, False)
-        weave_gpsimd(256, 256, rest)
-        x0.append((quantize(second, 128, "x0_1"), 0))
-        window = cast_pair(3)
-        wide = quantize(rest, 256, "x0_2", "raw3_0")
-        x0.extend([(wide, 0), (wide, 128)])
-        cast_w(0, nc.scalar.copy)
-        nc.vector.tensor_copy(picked1[:, :2, 1, :], window.indirect(offs_sb[:, :16]))
-        nc.vector.tensor_copy(picked1[:, 2, 1, :], window.indirect(offs_sb[:, 16:24]))
-        wq = [quantize(w_bf[:, 0].rearrange("p m j -> p (m j)"), N, "w0")]
-        nc.vector.tensor_copy(picked1[:, 3, 1, :], window.indirect(offs_sb[:, 24:]))
-        for a, j0, n in zip(acc, starts, PIECES):
-            product(a, wq[0], 0, x0[j0 // 128][0], x0[j0 // 128][1], n, True)
-        for copy, cols in ((nc.scalar.copy, slice(0, 64)), (nc.gpsimd.tensor_copy, slice(64, N))):
-            copy(w_bf[:, 1, cols, :], w_raw[1][:, :, cols].rearrange("p j m -> p m j"))
-        for i in range(3):
-            weave(picked1[:, i], 0, 128, woven1[i], False)
-        wq.append(quantize(w_bf[:, 1].rearrange("p m j -> p (m j)"), N, "w1"))
-        for a, j0, n in zip(acc, starts, PIECES):
-            product(a, wq[1], 0, quantize(woven1[j0 // 128], n, "x1_%d" % j0), 0, n, False)
-            if j0 == 0:
-                weave(picked1[:, 3], 0, 128, woven1[3], True)
-        for a, j0, n in zip(acc, starts, PIECES):
-            nc.scalar.activation(y[:, j0 : j0 + n], a[:], ACT.Gelu_apprx_tanh)
+        for i in range(PIECES):
+            product(acc[i], wq, 1, x1[i], 0)
+            nc.scalar.activation(y[:, i * PIECE : (i + 1) * PIECE], acc[i][:], ACT.Gelu_apprx_tanh)
 
         nb = [keep.tile([P, V], F32, name="nb%d" % i, align_bytes=64) for i in range(3)]
-        for t, pos in zip(nb, pos_sb):
-            nc.vector.tensor_copy(t[:], y[:].indirect(pos[:]))
+        halves = [slice(0, V // 2), slice(V // 2, V)]
+        for h in halves:
+            gather_v(nb[1][:, h], y, pos_sb[1], h.start, V // 2)
+        for i in (0, 2):
+            for h in halves:
+                gather_s(nb[i][:, h], y, pos_sb[i], h.start, V // 2)
         hi = keep.tile([P, V], F32, name="hi")
         lo = keep.tile([P, V], F32, name="lo")
         mid = keep.tile([P, V], F32, name="mid")
         med = keep.tile([P, V], F32, name="med")
-        halves = [slice(0, 96), slice(96, V)]
-        nc.vector.tensor_tensor(hi[:], nb[0][:], nb[1][:], ALU.max)
-        nc.vector.tensor_tensor(lo[:], nb[0][:], nb[1][:], ALU.min)
-        for h in halves:
-            nc.vector.tensor_tensor(mid[:, h], hi[:, h], nb[2][:, h], ALU.min)
+        a, b = halves
+        nc.vector.tensor_tensor(hi[:, a], nb[0][:, a], nb[1][:, a], ALU.max)
+        nc.vector.tensor_tensor(lo[:, a], nb[0][:, a], nb[1][:, a], ALU.min)
+        nc.vector.tensor_tensor(hi[:, b], nb[0][:, b], nb[1][:, b], ALU.max)
+        nc.vector.tensor_tensor(mid[:, a], hi[:, a], nb[2][:, a], ALU.min)
+        nc.vector.tensor_tensor(lo[:, b], nb[0][:, b], nb[1][:, b], ALU.min)
+        nc.vector.tensor_tensor(mid[:, b], hi[:, b], nb[2][:, b], ALU.min)
         for h in halves:
             nc.vector.tensor_tensor(med[:, h], lo[:, h], mid[:, h], ALU.max)
             nc.sync.dma_start(out=out[:, h], in_=med[:, h])

@@ -20,6 +20,7 @@ PASSES = K // (P * PACK)
 PIECE = 128
 PIECES = S // PIECE
 SHARES = (224, 224, 160)
+LOADS = ((2, 2), (1, 1, 1, 1))
 
 
 def tile_picked_median_gelu_e_kernel(tc, xT, w1, offs, pos1, pos2, pos3, out):
@@ -30,15 +31,20 @@ def tile_picked_median_gelu_e_kernel(tc, xT, w1, offs, pos1, pos2, pos3, out):
 
         offs_sb = keep.tile([P, S // 16], U16, name="offs_sb")
         pos_sb = [keep.tile([P, V // 16], U16, name="pos_sb%d" % i) for i in range(3)]
-        x_rows = xT.rearrange("(z p j) t -> z j p t", p=P, j=PACK)
+        x_rows = xT.rearrange("(z p j) t -> z p j t", p=P, j=PACK)
         w_rows = w1.rearrange("(z p j) m -> p z j m", p=P, j=PACK)
-        raw = [[keep.tile([P, T], F32, name="raw%d_%d" % (z, j), align_bytes=64) for j in range(PACK)] for z in range(PASSES)]
+        raw = []
         w_raw = keep.tile([P, PASSES, PACK, N], F32, name="w_raw", align_bytes=64)
         for z in range(PASSES):
-            for j in range(PACK):
-                nc.sync.dma_start(out=raw[z][j][:], in_=x_rows[z, j])
+            rows = []
+            for planes in LOADS[z]:
+                j = len(rows)
+                t = keep.tile([P, planes, T], F32, name="raw%d_%d" % (z, j), align_bytes=64)
+                nc.sync.dma_start(out=t[:], in_=x_rows[z, :, j : j + planes, :])
+                rows.extend(t[:, e, :] for e in range(planes))
                 if (z, j) == (0, 0):
                     nc.sync.dma_start(offs_sb[:], offs)
+            raw.append(rows)
             if z == 0:
                 nc.sync.dma_start(out=w_raw[:], in_=w_rows)
         for t, src in zip(pos_sb, (pos1, pos2, pos3)):
@@ -49,10 +55,10 @@ def tile_picked_median_gelu_e_kernel(tc, xT, w1, offs, pos1, pos2, pos3, out):
         nc.scalar.activation(warm[:, 1:2], warm[:, 0:1], ACT.Gelu_apprx_tanh)
 
         def gather_v(dst, window, offsets, j0, n):
-            nc.vector.tensor_copy(dst, window[:].indirect(offsets[:, j0 // 16 : (j0 + n) // 16]))
+            nc.vector.tensor_copy(dst, window.indirect(offsets[:, j0 // 16 : (j0 + n) // 16]))
 
         def gather_s(dst, window, offsets, j0, n):
-            nc.scalar.activation(dst, window[:].indirect(offsets[:, j0 // 16 : (j0 + n) // 16]), ACT.Copy)
+            nc.scalar.activation(dst, window.indirect(offsets[:, j0 // 16 : (j0 + n) // 16]), ACT.Copy)
 
         def quantize(src, n, name):
             codes = keep.tile([P, n], U32, name="codes_" + name, align_bytes=64)
@@ -70,7 +76,7 @@ def tile_picked_median_gelu_e_kernel(tc, xT, w1, offs, pos1, pos2, pos3, out):
 
         def front_pair(z, u, woven):
             share = SHARES[2 * z + u]
-            planes = keep.tile([P, 2, S - share], BF16, name="planes%d_%d" % (z, u), align_bytes=64)
+            planes = keep.tile([P, 2, S - share], BF16 if LOADS[z][0] == 1 else F32, name="planes%d_%d" % (z, u), align_bytes=64)
             for e in range(2):
                 gather_v(woven[:, :share, 2 * u + e], raw[z][2 * u + e], offs_sb, 0, share)
                 gather_s(planes[:, e, :], raw[z][2 * u + e], offs_sb, share, S - share)
@@ -114,10 +120,10 @@ def tile_picked_median_gelu_e_kernel(tc, xT, w1, offs, pos1, pos2, pos3, out):
         nb = [keep.tile([P, V], F32, name="nb%d" % i, align_bytes=64) for i in range(3)]
         halves = [slice(0, V // 2), slice(V // 2, V)]
         for h in halves:
-            gather_v(nb[1][:, h], y, pos_sb[1], h.start, V // 2)
+            gather_v(nb[1][:, h], y[:], pos_sb[1], h.start, V // 2)
         for i in (0, 2):
             for h in halves:
-                gather_s(nb[i][:, h], y, pos_sb[i], h.start, V // 2)
+                gather_s(nb[i][:, h], y[:], pos_sb[i], h.start, V // 2)
         hi = keep.tile([P, V], F32, name="hi")
         lo = keep.tile([P, V], F32, name="lo")
         mid = keep.tile([P, V], F32, name="mid")

@@ -19,8 +19,9 @@ PACK = 4
 PASSES = K // (P * PACK)
 PIECE = 128
 PIECES = S // PIECE
-SHARES = (224, 224, 160)
-LOADS = ((2, 2), (1, 1, 1, 1))
+SHARES = (224, 224)
+LAST_SHARE = 288
+LOADS = ((2, 1, 1), (1, 1, 1, 1))
 
 
 def tile_picked_median_gelu_e_kernel(tc, xT, w1, offs, pos1, pos2, pos3, out):
@@ -76,7 +77,7 @@ def tile_picked_median_gelu_e_kernel(tc, xT, w1, offs, pos1, pos2, pos3, out):
 
         def front_pair(z, u, woven):
             share = SHARES[2 * z + u]
-            planes = keep.tile([P, 2, S - share], BF16 if LOADS[z][0] == 1 else F32, name="planes%d_%d" % (z, u), align_bytes=64)
+            planes = keep.tile([P, 2, S - share], F32 if (z, u) == (0, 0) else BF16, name="planes%d_%d" % (z, u), align_bytes=64)
             for e in range(2):
                 gather_v(woven[:, :share, 2 * u + e], raw[z][2 * u + e], offs_sb, 0, share)
                 gather_s(planes[:, e, :], raw[z][2 * u + e], offs_sb, share, S - share)
@@ -93,25 +94,26 @@ def tile_picked_median_gelu_e_kernel(tc, xT, w1, offs, pos1, pos2, pos3, out):
             product(acc[i], wq, 0, x0, i * PIECE)
 
         woven1 = keep.tile([P, S, PACK], BF16, name="woven1", align_bytes=64)
-        front_pair(1, 0, woven1)
-        back = keep.tile([P, PIECES - 1, 2, PIECE], BF16, name="back", align_bytes=64)
+        near = keep.tile([P, 2, LAST_SHARE - PIECE], BF16, name="near", align_bytes=64)
+        far = keep.tile([P, 2, S - LAST_SHARE], BF16, name="far", align_bytes=64)
         for e in range(2):
-            gather_v(woven1[:, :PIECE, 2 + e], raw[1][2 + e], offs_sb, 0, PIECE)
-            for i in range(1, PIECES):
-                gather_s(back[:, i - 1, e, :], raw[1][2 + e], offs_sb, i * PIECE, PIECE)
-
-        def place(i, copy):
-            copy(woven1[:, i * PIECE : (i + 1) * PIECE, 2:4], back[:, i - 1].rearrange("p j n -> p n j"))
-
-        def quantize_piece(i):
-            return quantize(woven1[:, i * PIECE : (i + 1) * PIECE, :].rearrange("p n j -> p (n j)"), PIECE, "x1_%d" % i)
-
-        place(1, nc.vector.tensor_copy)
-        x1 = [quantize_piece(0)]
-        place(2, nc.vector.tensor_copy)
-        x1.append(quantize_piece(1))
-        place(3, nc.vector.tensor_copy)
-        x1.extend(quantize_piece(i) for i in range(2, PIECES))
+            gather_v(woven1[:, :PIECE, e], raw[1][e], offs_sb, 0, PIECE)
+            gather_s(near[:, e, :], raw[1][e], offs_sb, PIECE, LAST_SHARE - PIECE)
+            gather_s(far[:, e, :], raw[1][e], offs_sb, LAST_SHARE, S - LAST_SHARE)
+        nc.vector.tensor_copy(woven1[:, PIECE:LAST_SHARE, 0:2], near[:].rearrange("p j n -> p n j"))
+        nc.gpsimd.tensor_scalar(woven1[:, LAST_SHARE:, 0:2], far[:].rearrange("p j n -> p n j"), 1.0, 0.0, ALU.mult, ALU.add)
+        cuts = (LAST_SHARE, S - PIECE, S)
+        back = [keep.tile([P, 2, c1 - c0], BF16, name="back%d" % c0, align_bytes=64) for c0, c1 in zip(cuts, cuts[1:])]
+        for e in range(2):
+            for j0 in (0, PIECE):
+                n = PIECE if j0 == 0 else LAST_SHARE - PIECE
+                gather_v(woven1[:, j0 : j0 + n, 2 + e], raw[1][2 + e], offs_sb, j0, n)
+            for t, c0, c1 in zip(back, cuts, cuts[1:]):
+                gather_s(t[:, e, :], raw[1][2 + e], offs_sb, c0, c1 - c0)
+        for t, c0, c1 in zip(back, cuts, cuts[1:]):
+            nc.scalar.copy(woven1[:, c0:c1, 2:4], t[:].rearrange("p j n -> p n j"))
+        x1 = [quantize(woven1[:, i * PIECE : (i + 1) * PIECE, :].rearrange("p n j -> p (n j)"), PIECE, "x1_%d" % i)
+              for i in range(PIECES)]
         y = keep.tile([P, S], F32, name="y", align_bytes=64)
         for i in range(PIECES):
             product(acc[i], wq, 1, x1[i], 0)

@@ -20,7 +20,7 @@ PASSES = K // (P * PACK)
 PIECE = 128
 PIECES = S // PIECE
 SHARES = (224, 224)
-LAST_SHARE = 288
+LAST_SHARE = 224
 LOADS = ((2, 1, 1), (1, 1, 1, 1))
 
 
@@ -28,14 +28,16 @@ def tile_picked_median_gelu_e_kernel(tc, xT, w1, offs, pos1, pos2, pos3, out):
     nc = tc.nc
     with ExitStack() as ctx:
         keep = ctx.enter_context(tc.tile_pool(name="keep", bufs=1))
+        reuse = ctx.enter_context(tc.tile_pool(name="reuse", bufs=1))
         psum = ctx.enter_context(tc.psum_pool(name="psum", bufs=1))
 
         offs_sb = keep.tile([P, S // 16], U16, name="offs_sb")
         pos_sb = [keep.tile([P, V // 16], U16, name="pos_sb%d" % i) for i in range(3)]
         x_rows = xT.rearrange("(z p j) t -> z p j t", p=P, j=PACK)
-        w_rows = w1.rearrange("(z p j) m -> p z j m", p=P, j=PACK)
+        w_rows = w1.rearrange("(z p j) m -> z p j m", p=P, j=PACK)
         raw = []
-        w_raw = keep.tile([P, PASSES, PACK, N], F32, name="w_raw", align_bytes=64)
+        w_raw = [keep.tile([P, PACK, N], F32, name="w_raw0", align_bytes=64),
+                 reuse.tile([P, PACK, N], F32, name="w_raw1", align_bytes=64, offset=0)]
         for z in range(PASSES):
             rows = []
             for planes in LOADS[z]:
@@ -46,8 +48,7 @@ def tile_picked_median_gelu_e_kernel(tc, xT, w1, offs, pos1, pos2, pos3, out):
                 if (z, j) == (0, 0):
                     nc.sync.dma_start(offs_sb[:], offs)
             raw.append(rows)
-            if z == 0:
-                nc.sync.dma_start(out=w_raw[:], in_=w_rows)
+            nc.sync.dma_start(out=w_raw[z][:], in_=w_rows[z])
         for t, src in zip(pos_sb, (pos1, pos2, pos3)):
             nc.sync.dma_start(t[:], src)
 
@@ -61,19 +62,20 @@ def tile_picked_median_gelu_e_kernel(tc, xT, w1, offs, pos1, pos2, pos3, out):
         def gather_s(dst, window, offsets, j0, n):
             nc.scalar.activation(dst, window.indirect(offsets[:, j0 // 16 : (j0 + n) // 16]), ACT.Copy)
 
-        def quantize(src, n, name):
-            codes = keep.tile([P, n], U32, name="codes_" + name, align_bytes=64)
+        def quantize(src, n, name, codes=None):
+            if codes is None:
+                codes = keep.tile([P, n], U32, name="codes_" + name, align_bytes=64)[:]
             scales = keep.tile([P, n], U8, name="scales_" + name, align_bytes=64)
-            nc.vector.quantize_mx(out=codes[:].bitcast(FP8X4), scales=scales[:], in_=src)
+            nc.vector.quantize_mx(out=codes.bitcast(FP8X4), scales=scales[:], in_=src)
             return codes, scales
 
         def product(acc, wq, z, xq, c):
-            nc.tensor.matmul_mx(out=acc[:], lhsT=wq[0][:, z * N : (z + 1) * N].bitcast(FP8X4), lhsT_scale=wq[1][:, z * N : (z + 1) * N],
+            nc.tensor.matmul_mx(out=acc[:], lhsT=wq[0][:].bitcast(FP8X4), lhsT_scale=wq[1][:],
                                 rhs=xq[0][:, c : c + PIECE].bitcast(FP8X4), rhs_scale=xq[1][:, c : c + PIECE],
                                 start=z == 0, stop=z == PASSES - 1)
 
         acc = [psum.tile([P, PIECE], F32, name="acc%d" % i) for i in range(PIECES)]
-        w_bf = keep.tile([P, PASSES, N, PACK], BF16, name="w_bf", align_bytes=64)
+        w_bf = [keep.tile([P, N, PACK], BF16, name="w_bf%d" % z, align_bytes=64) for z in range(PASSES)]
 
         def front_pair(z, u, woven):
             share = SHARES[2 * z + u]
@@ -87,9 +89,8 @@ def tile_picked_median_gelu_e_kernel(tc, xT, w1, offs, pos1, pos2, pos3, out):
         front_pair(0, 0, woven0)
         front_pair(0, 1, woven0)
         x0 = quantize(woven0[:].rearrange("p n j -> p (n j)"), S, "x0")
-        nc.scalar.copy(w_bf[:, 0], w_raw[:, 0].rearrange("p j m -> p m j"))
-        nc.vector.tensor_copy(w_bf[:, 1], w_raw[:, 1].rearrange("p j m -> p m j"))
-        wq = quantize(w_bf[:].rearrange("p z m j -> p (z m j)"), PASSES * N, "w")
+        nc.scalar.copy(w_bf[0][:], w_raw[0][:].rearrange("p j m -> p m j"))
+        wq = quantize(w_bf[0][:].rearrange("p m j -> p (m j)"), N, "w0")
         for i in range(PIECES):
             product(acc[i], wq, 0, x0, i * PIECE)
 
@@ -105,15 +106,18 @@ def tile_picked_median_gelu_e_kernel(tc, xT, w1, offs, pos1, pos2, pos3, out):
         cuts = (LAST_SHARE, S - PIECE, S)
         back = [keep.tile([P, 2, c1 - c0], BF16, name="back%d" % c0, align_bytes=64) for c0, c1 in zip(cuts, cuts[1:])]
         for e in range(2):
-            for j0 in (0, PIECE):
-                n = PIECE if j0 == 0 else LAST_SHARE - PIECE
-                gather_v(woven1[:, j0 : j0 + n, 2 + e], raw[1][2 + e], offs_sb, j0, n)
+            gather_v(woven1[:, :LAST_SHARE, 2 + e], raw[1][2 + e], offs_sb, 0, LAST_SHARE)
             for t, c0, c1 in zip(back, cuts, cuts[1:]):
                 gather_s(t[:, e, :], raw[1][2 + e], offs_sb, c0, c1 - c0)
+        nc.vector.tensor_copy(w_bf[1][:], w_raw[1][:].rearrange("p j m -> p m j"))
         for t, c0, c1 in zip(back, cuts, cuts[1:]):
             nc.scalar.copy(woven1[:, c0:c1, 2:4], t[:].rearrange("p j n -> p n j"))
-        x1 = [quantize(woven1[:, i * PIECE : (i + 1) * PIECE, :].rearrange("p n j -> p (n j)"), PIECE, "x1_%d" % i)
-              for i in range(PIECES)]
+        x1 = []
+        for i in range(PIECES):
+            codes = reuse.tile([P, PIECE], U32, name="codes_x1_%d" % i, align_bytes=64, offset=4 * PIECE * i)
+            x1.append(quantize(woven1[:, i * PIECE : (i + 1) * PIECE, :].rearrange("p n j -> p (n j)"), PIECE, "x1_%d" % i, codes[:]))
+            if i == 0:
+                wq = quantize(w_bf[1][:].rearrange("p m j -> p (m j)"), N, "w1")
         y = keep.tile([P, S], F32, name="y", align_bytes=64)
         for i in range(PIECES):
             product(acc[i], wq, 1, x1[i], 0)

@@ -109,7 +109,7 @@ def tile_picked_median_gelu_e_kernel(tc, xT, w1, offs, pos1, pos2, pos3, out):
             gather_v(woven1[:, :LAST_SHARE, 2 + e], raw[1][2 + e], offs_sb, 0, LAST_SHARE)
             for t, c0, c1 in zip(back, cuts, cuts[1:]):
                 gather_s(t[:, e, :], raw[1][2 + e], offs_sb, c0, c1 - c0)
-        nc.vector.tensor_copy(w_bf[1][:], w_raw[1][:].rearrange("p j m -> p m j"))
+        nc.vector.tensor_copy(w_bf[1][:].rearrange("p (c i) j -> p c j i", i=4), w_raw[1][:].rearrange("p j (c i) -> p c j i", i=4))
         for t, c0, c1 in zip(back, cuts, cuts[1:]):
             nc.scalar.copy(woven1[:, c0:c1, 2:4], t[:].rearrange("p j n -> p n j"))
         x1 = []

@@ -21,7 +21,7 @@ PIECE = 128
 PIECES = S // PIECE
 SHARES = (224, 224)
 LAST_SHARE = 224
-LOADS = ((2, 1, 1), (1, 1, 1, 1))
+LOADS = ((1, 1, 1, 1), (1, 1, 1, 1))
 
 
 def tile_picked_median_gelu_e_kernel(tc, xT, w1, offs, pos1, pos2, pos3, out):
@@ -79,7 +79,7 @@ def tile_picked_median_gelu_e_kernel(tc, xT, w1, offs, pos1, pos2, pos3, out):
 
         def front_pair(z, u, woven):
             share = SHARES[2 * z + u]
-            planes = keep.tile([P, 2, S - share], F32 if (z, u) == (0, 0) else BF16, name="planes%d_%d" % (z, u), align_bytes=64)
+            planes = keep.tile([P, 2, S - share], BF16, name="planes%d_%d" % (z, u), align_bytes=64)
             for e in range(2):
                 gather_v(woven[:, :share, 2 * u + e], raw[z][2 * u + e], offs_sb, 0, share)
                 gather_s(planes[:, e, :], raw[z][2 * u + e], offs_sb, share, S - share)

@@ -19,7 +19,7 @@ PACK = 4
 PASSES = K // (P * PACK)
 PIECE = 128
 PIECES = S // PIECE
-SHARES = (224, 224)
+SHARES = (288, 288)
 LAST_SHARE = 224
 LOADS = ((1, 1, 1, 1), (1, 1, 1, 1))
 
@@ -77,31 +77,33 @@ def tile_picked_median_gelu_e_kernel(tc, xT, w1, offs, pos1, pos2, pos3, out):
         acc = [psum.tile([P, PIECE], F32, name="acc%d" % i) for i in range(PIECES)]
         w_bf = [keep.tile([P, N, PACK], BF16, name="w_bf%d" % z, align_bytes=64) for z in range(PASSES)]
 
-        def front_pair(z, u, woven):
+        def lay_g(dst, src):
+            nc.gpsimd.tensor_scalar(dst, src, 1.0, 0.0, ALU.mult, ALU.add)
+
+        def front_pair(z, u, woven, lay):
             share = SHARES[2 * z + u]
             planes = keep.tile([P, 2, S - share], BF16, name="planes%d_%d" % (z, u), align_bytes=64)
             for e in range(2):
                 gather_v(woven[:, :share, 2 * u + e], raw[z][2 * u + e], offs_sb, 0, share)
                 gather_s(planes[:, e, :], raw[z][2 * u + e], offs_sb, share, S - share)
-            nc.vector.tensor_copy(woven[:, share:, 2 * u : 2 * u + 2], planes[:].rearrange("p j n -> p n j"))
+            lay(woven[:, share:, 2 * u : 2 * u + 2], planes[:].rearrange("p j n -> p n j"))
 
         woven0 = keep.tile([P, S, PACK], BF16, name="woven0", align_bytes=64)
-        front_pair(0, 0, woven0)
-        front_pair(0, 1, woven0)
-        x0 = quantize(woven0[:].rearrange("p n j -> p (n j)"), S, "x0")
-        nc.scalar.copy(w_bf[0][:], w_raw[0][:].rearrange("p j m -> p m j"))
+        front_pair(0, 0, woven0, lay_g)
+        front_pair(0, 1, woven0, nc.scalar.copy)
+        x0 = (keep.tile([P, S], U32, name="codes_x0", align_bytes=64), keep.tile([P, S], U8, name="scales_x0", align_bytes=64))
+        for c in (slice(0, S // 2), slice(S // 2, S)):
+            nc.vector.quantize_mx(out=x0[0][:, c].bitcast(FP8X4), scales=x0[1][:, c], in_=woven0[:, c, :].rearrange("p n j -> p (n j)"))
+        lay_g(w_bf[0][:], w_raw[0][:].rearrange("p j m -> p m j"))
         wq = quantize(w_bf[0][:].rearrange("p m j -> p (m j)"), N, "w0")
         for i in range(PIECES):
             product(acc[i], wq, 0, x0, i * PIECE)
 
         woven1 = keep.tile([P, S, PACK], BF16, name="woven1", align_bytes=64)
-        near = keep.tile([P, 2, LAST_SHARE - PIECE], BF16, name="near", align_bytes=64)
         far = keep.tile([P, 2, S - LAST_SHARE], BF16, name="far", align_bytes=64)
         for e in range(2):
-            gather_v(woven1[:, :PIECE, e], raw[1][e], offs_sb, 0, PIECE)
-            gather_s(near[:, e, :], raw[1][e], offs_sb, PIECE, LAST_SHARE - PIECE)
+            gather_v(woven1[:, :LAST_SHARE, e], raw[1][e], offs_sb, 0, LAST_SHARE)
             gather_s(far[:, e, :], raw[1][e], offs_sb, LAST_SHARE, S - LAST_SHARE)
-        nc.vector.tensor_copy(woven1[:, PIECE:LAST_SHARE, 0:2], near[:].rearrange("p j n -> p n j"))
         nc.gpsimd.tensor_scalar(woven1[:, LAST_SHARE:, 0:2], far[:].rearrange("p j n -> p n j"), 1.0, 0.0, ALU.mult, ALU.add)
         cuts = (LAST_SHARE, S - PIECE, S)
         back = [keep.tile([P, 2, c1 - c0], BF16, name="back%d" % c0, align_bytes=64) for c0, c1 in zip(cuts, cuts[1:])]

from contextlib import ExitStack

import concourse.mybir as mybir

K, T, S, V, N = 1024, 1024, 512, 256, 128
FLOPS = 2 * K * N * S

F32 = mybir.dt.float32
BF16 = mybir.dt.bfloat16
U32 = mybir.dt.uint32
U16 = mybir.dt.uint16
U8 = mybir.dt.uint8
FP8X4 = mybir.dt.float8_e4m3fn_x4
ALU = mybir.AluOpType
ACT = mybir.ActivationFunctionType

P = 128
PACK = 4
PASSES = K // (P * PACK)
PIECE = 128
PIECES = S // PIECE
SHARES = (288, 288)
LAST_SHARE = 224
LOADS = ((1, 1, 1, 1), (1, 1, 1, 1))


def tile_picked_median_gelu_e_kernel(tc, xT, w1, offs, pos1, pos2, pos3, out):
    nc = tc.nc
    with ExitStack() as ctx:
        keep = ctx.enter_context(tc.tile_pool(name="keep", bufs=1))
        reuse = ctx.enter_context(tc.tile_pool(name="reuse", bufs=1))
        psum = ctx.enter_context(tc.psum_pool(name="psum", bufs=1))

        offs_sb = keep.tile([P, S // 16], U16, name="offs_sb")
        pos_sb = [keep.tile([P, V // 16], U16, name="pos_sb%d" % i) for i in range(3)]
        x_rows = xT.rearrange("(z p j) t -> z p j t", p=P, j=PACK)
        w_rows = w1.rearrange("(z p j) m -> z p j m", p=P, j=PACK)
        raw = []
        w_raw = [keep.tile([P, PACK, N], F32, name="w_raw0", align_bytes=64),
                 reuse.tile([P, PACK, N], F32, name="w_raw1", align_bytes=64, offset=0)]
        for z in range(PASSES):
            rows = []
            for planes in LOADS[z]:
                j = len(rows)
                t = keep.tile([P, planes, T], F32, name="raw%d_%d" % (z, j), align_bytes=64)
                nc.sync.dma_start(out=t[:], in_=x_rows[z, :, j : j + planes, :])
                rows.extend(t[:, e, :] for e in range(planes))
                if (z, j) == (0, 0):
                    nc.sync.dma_start(offs_sb[:], offs)
            raw.append(rows)
            nc.sync.dma_start(out=w_raw[z][:], in_=w_rows[z])
        for t, src in zip(pos_sb, (pos1, pos2, pos3)):
            nc.sync.dma_start(t[:], src)

        warm = keep.tile([P, 2], F32, name="warm")
        nc.gpsimd.memset(warm[:, 0:1], 0.0)
        nc.scalar.activation(warm[:, 1:2], warm[:, 0:1], ACT.Gelu_apprx_tanh)

        def gather_v(dst, window, offsets, j0, n):
            nc.vector.tensor_copy(dst, window.indirect(offsets[:, j0 // 16 : (j0 + n) // 16]))

        def gather_s(dst, window, offsets, j0, n):
            nc.scalar.activation(dst, window.indirect(offsets[:, j0 // 16 : (j0 + n) // 16]), ACT.Copy)

        def quantize(src, n, name, codes=None):
            if codes is None:
                codes = keep.tile([P, n], U32, name="codes_" + name, align_bytes=64)[:]
            scales = keep.tile([P, n], U8, name="scales_" + name, align_bytes=64)
            nc.vector.quantize_mx(out=codes.bitcast(FP8X4), scales=scales[:], in_=src)
            return codes, scales

        def product(acc, wq, z, xq, c):
            nc.tensor.matmul_mx(out=acc[:], lhsT=wq[0][:].bitcast(FP8X4), lhsT_scale=wq[1][:],
                                rhs=xq[0][:, c : c + PIECE].bitcast(FP8X4), rhs_scale=xq[1][:, c : c + PIECE],
                                start=z == 0, stop=z == PASSES - 1)

        acc = [psum.tile([P, PIECE], F32, name="acc%d" % i) for i in range(PIECES)]
        w_bf = [keep.tile([P, N, PACK], BF16, name="w_bf%d" % z, align_bytes=64) for z in range(PASSES)]

        def lay_g(dst, src):
            nc.gpsimd.tensor_scalar(dst, src, 1.0, 0.0, ALU.mult, ALU.add)

        def front_pair(z, u, woven, lay):
            share = SHARES[2 * z + u]
            planes = keep.tile([P, 2, S - share], BF16, name="planes%d_%d" % (z, u), align_bytes=64)
            for e in range(2):
                gather_v(woven[:, :share, 2 * u + e], raw[z][2 * u + e], offs_sb, 0, share)
                gather_s(planes[:, e, :], raw[z][2 * u + e], offs_sb, share, S - share)
            lay(woven[:, share:, 2 * u : 2 * u + 2], planes[:].rearrange("p j n -> p n j"))

        woven0 = keep.tile([P, S, PACK], BF16, name="woven0", align_bytes=64)
        front_pair(0, 0, woven0, lay_g)
        front_pair(0, 1, woven0, nc.scalar.copy)
        x0 = (keep.tile([P, S], U32, name="codes_x0", align_bytes=64), keep.tile([P, S], U8, name="scales_x0", align_bytes=64))
        for c in (slice(0, S // 2), slice(S // 2, S)):
            nc.vector.quantize_mx(out=x0[0][:, c].bitcast(FP8X4), scales=x0[1][:, c], in_=woven0[:, c, :].rearrange("p n j -> p (n j)"))
        lay_g(w_bf[0][:], w_raw[0][:].rearrange("p j m -> p m j"))
        wq = quantize(w_bf[0][:].rearrange("p m j -> p (m j)"), N, "w0")
        for i in range(PIECES):
            product(acc[i], wq, 0, x0, i * PIECE)

        woven1 = keep.tile([P, S, PACK], BF16, name="woven1", align_bytes=64)
        far = keep.tile([P, 2, S - LAST_SHARE], BF16, name="far", align_bytes=64)
        for e in range(2):
            gather_v(woven1[:, :LAST_SHARE, e], raw[1][e], offs_sb, 0, LAST_SHARE)
            gather_s(far[:, e, :], raw[1][e], offs_sb, LAST_SHARE, S - LAST_SHARE)
        nc.gpsimd.tensor_scalar(woven1[:, LAST_SHARE:, 0:2], far[:].rearrange("p j n -> p n j"), 1.0, 0.0, ALU.mult, ALU.add)
        cuts = (LAST_SHARE, S - PIECE, S)
        back = [keep.tile([P, 2, c1 - c0], BF16, name="back%d" % c0, align_bytes=64) for c0, c1 in zip(cuts, cuts[1:])]
        for e in range(2):
            gather_v(woven1[:, :LAST_SHARE, 2 + e], raw[1][2 + e], offs_sb, 0, LAST_SHARE)
            for t, c0, c1 in zip(back, cuts, cuts[1:]):
                gather_s(t[:, e, :], raw[1][2 + e], offs_sb, c0, c1 - c0)
        nc.vector.tensor_copy(w_bf[1][:].rearrange("p (c i) j -> p c j i", i=4), w_raw[1][:].rearrange("p j (c i) -> p c j i", i=4))
        for t, c0, c1 in zip(back, cuts, cuts[1:]):
            nc.scalar.copy(woven1[:, c0:c1, 2:4], t[:].rearrange("p j n -> p n j"))
        x1 = []
        for i in range(PIECES):
            codes = reuse.tile([P, PIECE], U32, name="codes_x1_%d" % i, align_bytes=64, offset=4 * PIECE * i)
            x1.append(quantize(woven1[:, i * PIECE : (i + 1) * PIECE, :].rearrange("p n j -> p (n j)"), PIECE, "x1_%d" % i, codes[:]))
            if i == 0:
                wq = quantize(w_bf[1][:].rearrange("p m j -> p (m j)"), N, "w1")
        y = keep.tile([P, S], F32, name="y", align_bytes=64)
        for i in range(PIECES):
            product(acc[i], wq, 1, x1[i], 0)
            nc.scalar.activation(y[:, i * PIECE : (i + 1) * PIECE], acc[i][:], ACT.Gelu_apprx_tanh)

        nb = [keep.tile([P, V], F32, name="nb%d" % i, align_bytes=64) for i in range(3)]
        halves = [slice(0, V // 2), slice(V // 2, V)]
        for h in halves:
            gather_v(nb[1][:, h], y[:], pos_sb[1], h.start, V // 2)
        for i in (0, 2):
            for h in halves:
                gather_s(nb[i][:, h], y[:], pos_sb[i], h.start, V // 2)
        hi = keep.tile([P, V], F32, name="hi")
        lo = keep.tile([P, V], F32, name="lo")
        mid = keep.tile([P, V], F32, name="mid")
        med = keep.tile([P, V], F32, name="med")
        a, b = halves
        nc.vector.tensor_tensor(hi[:, a], nb[0][:, a], nb[1][:, a], ALU.max)
        nc.vector.tensor_tensor(lo[:, a], nb[0][:, a], nb[1][:, a], ALU.min)
        nc.vector.tensor_tensor(hi[:, b], nb[0][:, b], nb[1][:, b], ALU.max)
        nc.vector.tensor_tensor(mid[:, a], hi[:, a], nb[2][:, a], ALU.min)
        nc.vector.tensor_tensor(lo[:, b], nb[0][:, b], nb[1][:, b], ALU.min)
        nc.vector.tensor_tensor(mid[:, b], hi[:, b], nb[2][:, b], ALU.min)
        for h in halves:
            nc.vector.tensor_tensor(med[:, h], lo[:, h], mid[:, h], ALU.max)
            nc.sync.dma_start(out=out[:, h], in_=med[:, h])
